import numpy as np, ml_dtypes
CORES = [7,391,135,263,15,399,143,271]
N = 8
R, T, B, CAPP = 8192, 2048, 64, 512
LOW = np.float32(-201 * 2.0 ** 92)
def entries(a): return a.T.reshape(-1)
def pack(v, P): return np.ascontiguousarray(np.asarray(v, np.int32).reshape(-1, P).T)
def table(rng, how, c=()):
    t = rng.standard_normal((N, 128, R), dtype=np.float32); k = np.arange(128) if how == "neg" else rng.permutation(128)[:16]
    t[:, k] = -0.125 - np.abs(t[:, k])
    if len(c): t[(c // R)[:, None], rng.permutation(128)[:16][None, :], (c % R)[:, None]] = LOW
    return t.astype(ml_dtypes.bfloat16)
def lists(rng, how):
    O = np.stack([rng.permutation(np.repeat(np.arange(N), CAPP))[:T] for r in range(N)])
    if how in ("astride", "early"): P = rng.permutation(N)[:T // CAPP]; O = np.stack([rng.permutation(np.repeat(P, CAPP)) for r in range(N)])
    I = R * O + rng.integers(0, R, (N, T))
    if how == "late": u = rng.random((N, T)); I = np.where(u < 0.5, R * O + np.where(u < 0.25, 0, R - 1), I)
    s = np.concatenate([[0], rng.integers(1 - T // 2, T // 2 + 1, N - 1), [int(rng.integers(1 - T // 2, 1))]])
    if how == "astride":
        z = int(rng.integers(1, N - 1)); k = int(rng.integers(0, B - 1)); s[1:z] = -rng.integers(1, T, z - 1); s[z] = -T; s[z + 1] = T; s[z + 2:N] = rng.integers(1, T, N - z - 2); s[N] = 0
    if how == "early": s[1:] = -T
    if how == "late": s[1:N] = T; s[N] = 0
    if how == "void":
        w = int(rng.integers(3, N - 1)); z = int(rng.integers(1, w - 1)); s[z] = int(rng.integers(1, T // 2 + 1)); s[z + 1] = s[z] - T; s[w:] = s[w] - T * np.arange(N + 1 - w)
    S = T * np.arange(N + 1) + s
    E = np.concatenate([np.append(np.sort(rng.integers(S[q], S[q + 1] + 1, B - 1)), S[q + 1]) for q in range(N)])
    if how == "astride":
        E[B * z:B * z + B - 1] = np.concatenate([np.sort(rng.integers(S[z], T * z - T // 2 + 1, k)), np.sort(rng.integers(T * z + T + T // 2, S[z + 1], B - 2 - k)), [S[z + 1] - 1]])
        L = max(N * T - 1, S[N - 1]); E[N * B - B:N * B - 1] = np.minimum(E[N * B - B:N * B - 1], L); E[N * B - 2] = L
        E += np.isin(E, np.setdiff1d(T * np.arange(1, N), S[z:z + 2]))
    if how == "neg":
        K = rng.random(N * B) < 0.5; K[0] = False; K[B - 1::B] = True; j = np.flatnonzero(K); E = E[j[np.searchsorted(j, np.arange(N * B))]]
    if how == "void":
        k = np.sort(np.stack([B * q + 1 + rng.permutation(B - 2)[:3] for q in range(N)]), axis=1); v = E[k]; v[:, 2] = S[1:]
        E = np.concatenate([[0], v.reshape(-1)])[np.searchsorted(k.reshape(-1), np.arange(N * B), side="right")]
    d = {"idx": np.stack([pack(i, 16) for i in I]), "end": np.stack([pack(E, 16)] * N)}
    if how == "neg":
        n = np.diff(np.concatenate([[0], E])).reshape(N, B); b = B * np.arange(N) + ((n > 0) * (1 + rng.random((N, B)))).argmax(axis=1)
        d["tab"] = table(rng, "neg", I.reshape(-1)[np.isin(np.searchsorted(E, np.arange(N * T), side="right"), b)])
    return d
def setup_inputs(rng):
    return dict({"tab": table(rng, "uniform")}, **lists(rng, "uniform"))
def setup_inputs_astride(rng):
    d = setup_inputs(rng); d.update(lists(rng, "astride"))
    for k in ("tab",): d[k] = (d[k].astype(np.float32) * 1048576.0).astype(d[k].dtype)
    return d
def setup_inputs_early(rng):
    d = setup_inputs(rng); d.update(lists(rng, "early"))
    for k in ("tab",): d[k] = (d[k].astype(np.float32) * (1 / 1024.0)).astype(d[k].dtype)
    return d
def setup_inputs_late(rng):
    d = setup_inputs(rng); d.update(lists(rng, "late"))
    return d
def setup_inputs_neg(rng):
    d = setup_inputs(rng); d.update(lists(rng, "neg"))
    return d
def setup_inputs_void(rng):
    d = setup_inputs(rng); d.update(lists(rng, "void"))
    return d
def check_inputs(x):
    bad = []
    if x["idx"].min() < 0 or x["idx"].max() >= N * R: bad.append("idx out of range")
    if x["end"].min() < 0 or x["end"].max() >= N * T + 1: bad.append("end out of range")
    if (x["end"] != x["end"][:1]).any(): bad.append("end differs from rank to rank")
    v = entries(x["end"][0]).astype(np.int64); s = v[B - 1::B]
    if (np.diff(v) < 0).any(): bad.append("end falls")
    if any(s[q - 1] > T * (q + 1) or (s[q - 1] < T * (q - 1) and s[q - 1] != s[N - 1]) for q in range(1, N)): bad.append("an entry belongs to a bag of a rank that is more than one away from its holder")
    if max(int(np.bincount(entries(a) // R, minlength=N).max()) for a in x["idx"]) > CAPP: bad.append("more than CAPP entries of a rank's idx point into one rank's part of the table")
    t = x["tab"].astype(np.float32)
    if t.min() < np.float32(-1e30) or t.max() > np.float32(1e30): bad.append("tab beyond -1e30 to 1e30")
    return bad
def reference(tab, idx, end):
    A = np.concatenate(list(tab), axis=1)
    G = A[:, np.concatenate([entries(a) for a in idx])]
    Y = np.zeros((128, N * B), tab.dtype)
    for r in range(N):
        c = np.concatenate([[0], entries(end[r])])
        for b in range(B * r, B * r + B):
            if c[b + 1] > c[b]: Y[:, b] = G[:, c[b]:c[b + 1]].max(axis=1)
    return {"y": np.stack([Y[:, B * r:B * r + B] for r in range(N)])}

@@ -1,0 +1,445 @@
+from concourse.bass import DstId, RemoteDMATransfer
+from concourse.mybir import dt, AluOpType as A, AxisListType, ActivationFunctionType as F
+
+N, RC, NB, CAP = 8, 8192, 64, 512
+BIG = 201.0 * 2.0 ** 92
+LOW = -BIG
+SC0 = 16
+
+DT = {"f": "float32", "b": "bfloat16", "i": "int32", "u": "uint16"}
+SBUF = "tabS:8208:b Gt:4096:b SC:4112:b FS:4096:b R:512:f O:512:b P:512:b yS:64:b I:128:i E:32:i EP:4:i Es:4096:b oA:2048:b oL:1024:b Gm:512:f"
+SMALL = """mx:512:b ownI:128:i ownB:128:b IF:128:f EI:128:i EF:64:b EPI:8:i inr:8:f QE:12:f Q:12:f ge:4:f KI:8:i KF:8:f io128:128:b
+im16:128:b id16:128:b ones:512:b BO:128:b Tri:128:b TriU:128:b Ob:8:f Rep:128:b S16:16:f Sel:128:f m33:32:f m32:32:f LW:512:f Sh:384:f
+Mb:136:b Cb:136:b X:128:f DP:128:b LI:64:i LF:48:f PI:48:i PF:48:f oB:512:b Tt:512:b mP:512:b off:256:u BI:12:i BF:8:f hA:512:b
+hC:128:b Fl:128:b xe:16:f xr:128:f xo:32:u"""
+SCRATCH, PLACE, _w = {}, {}, {}
+for _t in SBUF.split():
+    _n, _c, _d = _t.split(":")
+    SCRATCH[_n] = ("sbuf", [128, int(_c)], DT[_d])
+    PLACE[_n] = (_n, 0)
+for _t in SMALL.split():
+    _n, _c, _d = _t.split(":")
+    PLACE[_n] = ("small_" + _d, _w.get(_d, 0))
+    _w[_d] = _w.get(_d, 0) + (int(_c) + 15) // 16 * 16
+for _d in _w:
+    SCRATCH["small_" + _d] = ("sbuf", [128, _w[_d]], DT[_d])
+for _i in range(8):
+    SCRATCH["b%d" % _i] = ("psum", [128, 512], "float32")
+    PLACE["b%d" % _i] = ("b%d" % _i, 0)
+SEMAPHORES = "sv ss sp sg dI dT dE dP dY la ld pa pd0 pd1 r1 r2 r3 sent".split()
+CACHE = {}
+
+
+def plan(cores, topo):
+    if "p" in CACHE:
+        return CACHE["p"]
+    rel, far, used = {}, {}, set(cores)
+    for r, c in enumerate(cores):
+        far[r] = [q for q in range(N) if q != r and not topo.may_write(c, cores[q])]
+        best = None
+        for x in range(512):
+            if x in used or topo.rack(topo.host(x)) == topo.rack(topo.host(c)) or topo.chip(x) != topo.chip(c):
+                continue
+            if not topo.may_write(c, x) or not all(topo.may_write(x, cores[q]) for q in far[r]):
+                continue
+            k = (topo.die(x) == topo.die(c), x)
+            if best is None or k < best:
+                best = k
+        rel[r] = best[1]
+        used.add(best[1])
+    CACHE["p"] = (rel, far)
+    return CACHE["p"]
+
+
+def bits(mask, a, n):
+    return sum([1 << i for i in range(16) if mask >> i & 1][a:a + n])
+
+
+def half_plan(r, far, half):
+    d = [q for q in range(4 * half, 4 * half + 4) if q != r and q not in far[r]]
+    out, a = [], 0
+    for q, n in zip(d, {2: [4, 4], 3: [2, 2, 4]}[len(d)]):
+        out.append((q, a, n))
+        a += n
+    return out
+
+
+def position(q, far):
+    near = [s for s in range(N) if s not in far[q]]
+    return {s: i for i, s in enumerate(near + far[q])}
+
+
+def rank_program(g, core, T, topo):
+    cores = list(T.cores)
+    rel, far = plan(cores, topo)
+    me = T.rank_of(core)
+
+    def dst(c):
+        rid, pid = topo.addr(c, core)
+        return DstId(rid=rid, pnc=pid)
+
+    def xfer(src, to, dname, c0, c1, sem, eng=(0, 8)):
+        m = topo.mask(core, to[0])
+        for c in to[1:]:
+            m = m & topo.mask(core, c)
+        return RemoteDMATransfer(srcs=[src], dsts=[T[dname][:, c0:c1] for _ in to], dst_ids=[dst(c) for c in to],
+                                 dma_engine_mask=bits(m, eng[0], eng[1]), remote_sem=T.sem[sem])
+
+    if me is None:
+        for s in range(N):
+            if rel[s] == core:
+                q0, q1 = far[s]
+                g.wait_ge(T.sem.r1, 8)
+                g.remote_dma_fused([xfer(T.R[:, 64 * s:64 * s + 64], [cores[q0], cores[q1]], "R", 64 * s, 64 * s + 64, "ld")], local_sem=T.sem.sent)
+                for i, q in enumerate((q0, q1)):
+                    g.wait_ge(T.sem[("r2", "r3")[i]], 8)
+                    p = position(q, far)[s]
+                    g.remote_dma_fused([xfer(T.O[:, 64 * i:64 * i + 64], [cores[q]], "P", 64 * p, 64 * p + 64, "pd%d" % (p - 6))], local_sem=T.sem.sent)
+                g.wait_ge(T.sem.sent, 24)
+        return
+
+    Q = {"v": g.vector, "s": g.scalar, "p": g.tensor, "g": g, "y": g.sync}
+    cnt = {"v": 0, "s": 0, "p": 0, "g": 0}
+    seen, acc = {}, {}
+
+    def R(name, c0, c1, p0=0, p1=128, step=1):
+        b, o = PLACE[name]
+        return (b, p0, p1, c0 + o, c1 + o, step)
+
+    def ap(r):
+        return T[r[0]][r[1]:r[2], r[3]:r[4]] if r[5] == 1 else T[r[0]][r[1]:r[2], r[3]:r[4]:r[5]]
+
+    def col(name, c, p0=0, p1=128):
+        return R(name, c, c + 1, p0, p1)
+
+    def depend(q, outs, ins):
+        want = {}
+        for kind, regs in (("w", outs), ("r", ins)):
+            for r in regs:
+                bank = SCRATCH[r[0]][0] == "psum"
+                for (r2, k2, tok, q2) in acc.get(r[0], []):
+                    if bank and q2 != q:
+                        hit = True
+                    elif bank and q == "p":
+                        hit = False
+                    else:
+                        hit = r[1] < r2[2] and r2[1] < r[2] and r[3] < r2[4] and r2[3] < r[4] and (kind == "w" or k2 == "w")
+                        if q == q2 and k2 == "r":
+                            hit = False
+                    if hit and want.get(tok[0], 0) < tok[1]:
+                        want[tok[0]] = tok[1]
+        for s in want:
+            if seen.get((q, s), 0) < want[s]:
+                Q[q].wait_ge(T.sem[s], want[s])
+                seen[(q, s)] = want[s]
+
+    def note(q, outs, ins, tok):
+        for kind, regs in (("w", outs), ("r", ins)):
+            for r in regs:
+                acc.setdefault(r[0], []).append((r, kind, tok, q))
+
+    def run(q, fn, outs, ins):
+        depend(q, outs, ins)
+        cnt[q] += 1
+        tok = ("s" + q, cnt[q])
+        fn().then_inc(T.sem[tok[0]], 1)
+        note(q, outs, ins, tok)
+
+    def val(x):
+        return ap(x) if isinstance(x, tuple) else x
+
+    def ts(out, in0, s1, op0, s2=None, op1=None):
+        ins = [in0] + [s for s in (s1, s2) if isinstance(s, tuple)]
+        if op1 is None:
+            run("v", lambda: g.vector.tensor_scalar(ap(out), ap(in0), val(s1), None, op0), [out], ins)
+        else:
+            run("v", lambda: g.vector.tensor_scalar(ap(out), ap(in0), val(s1), val(s2), op0, op1), [out], ins)
+
+    def tt(out, a, b, op):
+        run("v", lambda: g.vector.tensor_tensor(ap(out), ap(a), ap(b), op), [out], [a, b])
+
+    def cp(out, a):
+        run("v", lambda: g.vector.tensor_copy(ap(out), ap(a)), [out], [a])
+
+    def fill(r, c):
+        run("v", lambda: g.vector.memset(ap(r), c), [r], [])
+
+    def scan(out, d0, d1, ini, op0, op1):
+        run("v", lambda: g.vector.tensor_tensor_scan(ap(out), ap(d0), ap(d1), val(ini), op0, op1), [out], [d0, d1] + ([ini] if isinstance(ini, tuple) else []))
+
+    def act(out, a, func, scale=1.0, bias=0.0):
+        ins = [a] + [s for s in (scale, bias) if isinstance(s, tuple)]
+        if isinstance(bias, tuple):
+            run("s", lambda: g.scalar.activation(ap(out), ap(a), func, bias=val(bias), scale=val(scale)), [out], ins)
+        else:
+            run("s", lambda: g.scalar.activation(ap(out), ap(a), func, scale=val(scale)), [out], ins)
+
+    def mm(out, lhsT, rhs, start=True, stop=True):
+        run("p", lambda: g.tensor.matmul(ap(out), ap(lhsT), ap(rhs), start, stop), [out], [lhsT, rhs])
+
+    def iota(out, pattern, cm=0):
+        if SCRATCH[out[0]][2] == "int32":
+            run("g", lambda: g.iota(ap(out), pattern, 0, cm), [out], [])
+        else:
+            run("g", lambda: g.iota(ap(out), pattern, 0, cm, allow_small_or_imprecise_dtypes=True), [out], [])
+
+    def load(q, out, src, sem, v):
+        Q[q].dma_start(ap(out), src).then_inc(T.sem[sem], 16)
+        note("d" + sem, [out], [], (sem, v))
+
+    def indirect(q, out, win, off):
+        if q == "s":
+            run("s", lambda: g.scalar.activation(ap(out), ap(win).indirect(ap(off)), F.Copy), [out], [win, off])
+        else:
+            run("v", lambda: g.vector.tensor_copy(ap(out), ap(win).indirect(ap(off))), [out], [win, off])
+
+    load("y", R("I", 0, 128, 0, 16), T.idx[:, :], "dI", 16)
+    load("s", R("E", 0, 32, 0, 16), T.end[:, :], "dE", 16)
+    for w in range(4):
+        load("ys"[w % 2], col("EP", w), T.end[4 * w:4 * w + 4, :], "dP", 64)
+    load("y", R("tabS", 0, RC), T.tab[:, :], "dT", 16)
+
+    iota(col("KI", 0), [[0, 1]], 1)
+    iota(R("im16", 0, 128), [[0, 8], [1, 16]])
+    iota(R("id16", 0, 128), [[1, 8], [0, 16]])
+    iota(R("io128", 0, 128), [[1, 128]])
+    fill(R("ones", 0, 512), 1.0)
+    fill(R("Mb", 0, 8), 0.0)
+    fill(R("Cb", 0, 8), 0.0)
+    for i, (n, op) in enumerate(((15, A.bitwise_and), (4, A.arith_shift_right), (31, A.bitwise_and), (5, A.arith_shift_right))):
+        ts(col("KI", 1 + i), col("KI", 0), n, op)
+    cp(R("KF", 0, 5), R("KI", 0, 5))
+    kk, kp, kg, km, kd = [col("KF", i) for i in range(5)]
+    ts(R("Rep", 0, 128), R("im16", 0, 128), kp, A.is_equal)
+    ts(R("S16", 0, 16), R("im16", 0, 16), kp, A.is_equal)
+    ts(R("BO", 0, 128), R("id16", 0, 128), kg, A.is_equal)
+    fill(R("m33", 0, 32, 32, 33), 1.0)
+    ts(R("m33", 0, 32, 0, 32), R("io128", 0, 32, 0, 32), col("KF", 0, 0, 32), A.is_equal)
+    ts(R("Tri", 0, 128), R("io128", 0, 128), kk, A.is_ge)
+    tt(R("Tri", 0, 128), R("Tri", 0, 128), R("BO", 0, 128), A.mult)
+    tt(R("TriU", 0, 128), R("BO", 0, 128), R("Tri", 0, 128), A.subtract)
+    ts(col("KF", 5), kk, -1.0, A.mult, 0.5, A.add)
+    ts(col("KF", 6), kg, float(me), A.is_equal)
+
+    def selectors(c0, c1):
+        for c in range(c0, c1):
+            act(R("Es", 128 * c, 128 * c + 128, 0, 33), R("ones", 0, 128, 0, 33), F.Copy, scale=col("m33", c, 0, 33))
+
+    selectors(0, 16)
+
+    ts(R("ownI", 0, 128, 0, 16), R("I", 0, 128, 0, 16), 13, A.arith_shift_right)
+    cp(R("ownB", 0, 128, 0, 16), R("ownI", 0, 128, 0, 16))
+    mm(R("b0", 0, 128), R("Rep", 0, 128, 0, 16), R("ownB", 0, 128, 0, 16))
+    cp(R("IF", 0, 128, 0, 16), R("I", 0, 128, 0, 16))
+    mm(R("b1", 0, 16), R("IF", 0, 128, 0, 16), R("S16", 0, 16, 0, 16))
+    ts(R("EI", 0, 32, 0, 16), R("E", 0, 32, 0, 16), -1.0, A.add)
+    ts(R("EI", 32, 64, 0, 16), R("EI", 0, 32, 0, 16), 4, A.arith_shift_right)
+    ts(R("Mb", 8, 136), R("b0", 0, 128), kg, A.is_equal)
+    scan(R("Cb", 8, 136), R("ones", 0, 128), R("Mb", 8, 136), 0.0, A.mult, A.add)
+    mm(R("b2", 0, 128), R("Tri", 0, 128), R("Mb", 8, 136), True, False)
+    mm(R("b2", 0, 128), R("BO", 0, 128), R("Cb", 7, 135), False, True)
+    ts(R("EI", 64, 96, 0, 16), R("EI", 32, 64, 0, 16), float(-128 * me), A.add, -1.0, A.max)
+    ts(R("EI", 96, 128, 0, 16), R("EI", 0, 32, 0, 16), 15, A.bitwise_and)
+    ts(R("EF", 0, 32, 0, 16), R("EI", 64, 96, 0, 16), 128.0, A.min)
+    cp(R("EF", 32, 64, 0, 16), R("EI", 96, 128, 0, 16))
+    tt(R("X", 0, 128), R("b2", 0, 128), R("Mb", 8, 136), A.mult)
+    mm(R("b4", 0, 16), R("X", 0, 128), R("S16", 0, 16))
+    mm(R("b3", 0, 128), R("Mb", 8, 136), R("Tri", 0, 128), True, False)
+    mm(R("b3", 0, 128), R("Mb", 7, 135), R("TriU", 0, 128), False, True)
+    cp(R("LI", 0, 16), R("b1", 0, 16))
+    ts(R("LI", 16, 32), R("LI", 0, 16), 127, A.bitwise_and)
+    ts(R("LI", 32, 48), R("LI", 0, 16), 7, A.arith_shift_right, 63, A.bitwise_and)
+    ts(R("LI", 48, 64), R("LI", 0, 16), 13, A.arith_shift_right)
+    ts(R("PI", 0, 16), R("b4", 0, 16), -1.0, A.add)
+    ts(R("PI", 16, 32), R("PI", 0, 16), 15, A.bitwise_and)
+    ts(R("PI", 32, 48), R("PI", 0, 16), 4, A.arith_shift_right)
+    ts(R("LF", 32, 48), R("LI", 48, 64), 16.0, A.mult)
+    cp(R("PF", 0, 32), R("PI", 16, 48))
+    tt(R("PF", 32, 48), R("PF", 0, 16), R("LF", 32, 48), A.add)
+    cp(R("LF", 0, 16), R("LI", 16, 32))
+    ts(R("LF", 16, 32), R("LI", 32, 48), -64.0, A.add, 128.0, A.mult)
+    act(R("DP", 0, 128), R("b3", 0, 128), F.Copy)
+    for h in range(2):
+        for p in range(16):
+            mm(R(("b6", "b7")[h], 32 * p, 32 * p + 32), R("Es", 128 * p, 128 * p + 128, 0, 16), R("EF", 32 * h, 32 * h + 32, 0, 16))
+    for p in range(16):
+        ts(R("oB", 32 * p, 32 * p + 32), R("io128", 0, 32), col("PF", 16 + p), A.is_equal)
+        ts(R("oA", 128 * p, 128 * p + 128), R("io128", 0, 128), col("PF", 32 + p), A.is_equal)
+        if p == 8:
+            act(R("Tt", 0, 512), R("b6", 0, 512), F.Sign, bias=col("KF", 5))
+            mm(R("b0", 0, 512), R("DP", 0, 128), R("ones", 0, 512), True, False)
+            mm(R("b0", 0, 512), R("DP", 0, 128), R("Tt", 0, 512), False, True)
+            ts(R("mP", 0, 512), R("b7", 0, 512), kp, A.is_equal)
+            ts(R("Ob", 0, 8), R("io128", 0, 8), kg, A.is_equal)
+            ts(R("EPI", 0, 4), R("EP", 0, 4), -1.0, A.add)
+            ts(R("EPI", 4, 8), R("EPI", 0, 4), 11, A.arith_shift_right)
+            ts(R("inr", 0, 4), R("EPI", 4, 8), float(me), A.is_equal, 0.5, A.mult)
+            ts(R("inr", 4, 8), R("EPI", 4, 8), float(me), A.is_equal, float(CAP * me), A.mult)
+        if p == 12:
+            tt(R("Gm", 0, 512), R("b0", 0, 512), R("mP", 0, 512), A.mult)
+            for w in range(4):
+                mm(R("b2", 8 * w, 8 * w + 8), R("Gm", 128 * w, 128 * w + 128), R("Ob", 0, 8))
+        for h in range(2):
+            act(R("oL", 64 * p + 32 * h, 64 * p + 32 * h + 32), R("oB", 32 * p, 32 * p + 32), F.Copy, scale=col("LF", 16 * h + p))
+        for h in range(2):
+            mm(R("b5", 0, 32), R("oA", 128 * p, 128 * p + 128), R("oL", 64 * p + 32 * h, 64 * p + 32 * h + 32), p == 0 and h == 0, p == 15 and h == 1)
+    r0 = 64 * me
+    for w in range(4):
+        act(R("R", r0 + 1 + 16 * w, r0 + 16 * w + 16, step=2), R("b2", 8 * w, 8 * w + 8), F.Identity, scale=col("inr", w), bias=col("inr", 4 + w))
+    cp(R("R", r0, r0 + 63, step=2), R("b5", 0, 32))
+    selectors(16, 32)
+
+    own = R("R", r0, r0 + 64)
+    depend("g", [], [own])
+    g.remote_dma_fused([xfer(ap(own), [rel[me]], "R", r0, r0 + 64, "r1")], local_sem=T.sem.sent)
+    near = [q for q in range(N) if q != me and q not in far[me]]
+    g.remote_dma_fused([xfer(ap(own), [cores[q] for q in near], "R", r0, r0 + 64, "la")], local_sem=T.sem.sent)
+    for s in range(N):
+        if s != me:
+            note("n", [R("R", 64 * s, 64 * s + 64)], [], ("ld", 16) if s in far[me] else ("la", 8 * len(near)))
+
+    ts(R("Sel", 0, 128), R("im16", 0, 128), kp, A.is_equal, col("KF", 6), A.mult)
+    fill(R("tabS", RC, RC + 16), LOW)
+    fill(R("SC", 0, SC0), LOW)
+    fill(R("SC", 1, 2), 0.0)
+    fill(R("Fl", 0, 128, 32, 33), BIG)
+    fill(col("KF", 7), BIG)
+    ts(col("KF", 7), col("KF", 7), -2.0, A.mult)
+    ts(R("m32", 0, 32), R("io128", 0, 32), km, A.is_equal)
+    for w in range(4):
+        ts(R("LW", 128 * w, 128 * w + 128), R("im16", 0, 128), kd, A.subtract, 4.0 * w, A.is_equal)
+    for i, d in enumerate((32.0, -96.0, -95.0)):
+        ts(R("Sh", 128 * i, 128 * i + 128), R("io128", 0, 128), kk, A.subtract, d, A.is_equal)
+    fill(R("Sh", 256, 257), 0.0)
+    fill(R("Sh", 288, 289), 0.0)
+    fill(R("QE", 0, 12), 0.0)
+    fill(R("Q", 0, 12), 0.0)
+
+    def before(q):
+        cp(R(q, 5, 8), R(q, 0, 3))
+        cp(R(q, 8, 9), R(q, 3, 4))
+        for i in range(3):
+            mm(R("b7", 0, 4), R("Sh", 128 * i, 128 * i + 128), R(q, 4 * i, 4 * i + 4), i == 0, i == 2)
+
+    cp(R("QE", 0, 4), R("EP", 0, 4))
+    before("QE")
+    tt(R("ge", 0, 4), R("QE", 0, 4), R("b7", 0, 4), A.is_le)
+
+    def offsets(ss, bank):
+        runs = []
+        for s in ss:
+            if runs and runs[-1][1] == s:
+                runs[-1][1] = s + 1
+            else:
+                runs.append([s, s + 1])
+        for a, b in runs:
+            mm(R(bank, 32 * a, 32 * b), R("Sel", 0, 128), R("R", 64 * a, 64 * b - 1, step=2))
+        for a, b in runs:
+            ts(R("off", 32 * a, 32 * b), R(bank, 32 * a, 32 * b), float(RC), A.add)
+
+    def gather(q, s):
+        indirect(q, R("Gt", CAP * s, CAP * s + CAP), R("tabS", 0, RC + 16), R("off", 32 * s, 32 * s + 32))
+
+    direct = [s for s in range(N) if s not in far[me]]
+    offsets(direct, "b1")
+    for i, s in enumerate(direct):
+        gather("sv"[i % 2], s)
+    offsets(far[me], "b4")
+    for s in far[me]:
+        gather("s", s)
+
+    for w in range(4):
+        c = 1 + 2 * (8 * w + me)
+        src, out = R("R", c, 64 * 7 + c + 1, step=64), col("Q", w)
+        run("v", lambda: g.vector.tensor_reduce(ap(out), ap(src), AxisListType.X, A.add), [out], [src])
+    before("Q")
+    cp(R("BI", 0, 4), R("Q", 0, 4))
+    ts(R("BI", 4, 8), R("BI", 0, 4), 127, A.bitwise_and)
+    ts(R("BI", 8, 12), R("BI", 0, 4), 7, A.arith_shift_right)
+    cp(R("BF", 0, 8), R("BI", 4, 12))
+    for w in range(4):
+        ts(R("hA", 128 * w, 128 * w + 128), R("io128", 0, 128), col("BF", w), A.is_equal)
+        ts(R("hC", 32 * w, 32 * w + 32), R("io128", 0, 32), col("BF", 4 + w), A.is_equal)
+        mm(R("b2", 0, 128, 0, 32), R("hC", 32 * w, 32 * w + 32), R("hA", 128 * w, 128 * w + 128), w == 0, w == 3)
+    tt(R("xe", 0, 4), R("Q", 0, 4), R("b7", 0, 4), A.is_gt)
+    ts(R("xe", 4, 8), R("Q", 0, 4), float(SC0 - 1), A.add)
+    tt(R("xe", 8, 12), R("xe", 0, 4), R("xe", 4, 8), A.mult)
+    tt(R("xe", 12, 16), R("xe", 8, 12), R("ge", 0, 4), A.add)
+    ts(R("Fl", 0, 128, 0, 32), R("b2", 0, 128, 0, 32), 1.0, A.min, col("KF", 7, 0, 32), A.mult)
+    banks = ["b0", "b3", "b5", "b6", "b7", "b1", "b4", "b0"]
+
+    def flags(i):
+        for c in range(4 * i, 4 * i + 4):
+            mm(R(banks[i], 128 * (c % 4), 128 * (c % 4) + 128), R("Es", 128 * c, 128 * c + 128, 0, 33), R("Fl", 0, 128, 0, 33))
+
+    for i in range(4):
+        flags(i)
+    for w in range(4):
+        ts(R("xr", 32 * w, 32 * w + 32), R("m32", 0, 32), col("xe", 12 + w), A.mult)
+        mm(R("b2", 0, 32), R("LW", 128 * w, 128 * w + 128), R("xr", 32 * w, 32 * w + 32), w == 0, w == 3)
+    pos = position(me, far)
+    slot = {q: i for i, q in enumerate(far[me])}
+    for q in range(N):
+        if q not in slot and q != me:
+            slot[q] = len(slot)
+
+    def piece(q):
+        return R("O", 64 * slot[q], 64 * slot[q] + 64)
+
+    def take(e, q, top):
+        o = R("P", 64 * pos[me], 64 * pos[me] + 64) if q == me else piece(q)
+        indirect(e, o, R("SC", 0, SC0 + CAP * top), R("xo", 4 * q, 4 * q + 4))
+
+    def send(half):
+        q = far[me][half]
+        depend("g", [], [piece(q)])
+        g.remote_dma_fused([xfer(ap(piece(q)), [rel[me]], "O", 64 * half, 64 * half + 64, ("r2", "r3")[half])], local_sem=T.sem.sent)
+        tr, n = [], 0
+        for q, a, k in half_plan(me, far, half):
+            depend("g", [], [piece(q)])
+            p = position(q, far)[me]
+            tr.append(xfer(ap(piece(q)), [cores[q]], "P", 64 * p, 64 * p + 64, "pa", (a, k)))
+            n += k
+        g.remote_dma_fused(tr, local_sem=T.sem.sent)
+        return 8 + n
+
+    def order(half):
+        return sorted(range(4 * half, 4 * half + 4), key=lambda q: (q not in far[me], q == me, q))
+
+    n = 16
+    for i in range(N):
+        g0, g1 = CAP * i, CAP * i + CAP
+        fl = R(banks[i], 0, 512)
+        if i in (2, 4):
+            act(R("FS", g0, g1), fl, F.Copy)
+            fl = R("FS", g0, g1)
+        last = R("SC", SC0 + g0 - 1, SC0 + g0)
+        scan(R("SC", SC0 + g0, SC0 + g1), fl, R("Gt", g0, g1), last if i else LOW, A.min, A.max)
+        if i + 4 < N:
+            flags(i + 4)
+        if i == 2:
+            cp(R("xo", 0, 32), R("b2", 0, 32))
+        if i == 4:
+            for q in order(0):
+                take("s", q, 5)
+            n += send(0)
+    for j, q in enumerate(order(1)):
+        take("vs"[j % 2], q, 8)
+    n += send(1)
+
+    exp = sum(k for s in range(N) for half in range(2) for q, a, k in half_plan(s, far, half) if q == me)
+    note("n", [R("P", 64 * pos[s], 64 * pos[s] + 64) for s in direct if s != me], [], ("pa", exp))
+    for i in range(2):
+        note("n", [R("P", 64 * (6 + i), 64 * (7 + i))], [], ("pd%d" % i, 8))
+    tt(R("mx", 0, 192), R("P", 0, 192), R("P", 192, 384), A.max)
+    tt(R("mx", 192, 256), R("mx", 0, 64), R("mx", 64, 128), A.max)
+    tt(R("mx", 256, 320), R("mx", 192, 256), R("mx", 128, 192), A.max)
+    tt(R("mx", 320, 384), R("P", 384, 448), R("P", 448, 512), A.max)
+    tt(R("yS", 0, 64), R("mx", 256, 320), R("mx", 320, 384), A.max)
+    depend("y", [], [R("yS", 0, 64)])
+    g.sync.dma_start(T.y[:, :], T.yS[:, :]).then_inc(T.sem.dY, 16)
+    g.sync.wait_ge(T.sem.dY, 16)
+    g.wait_ge(T.sem.sent, n)
+    for s in "vspg":
+        if seen.get(("g", "s" + s), 0) < cnt[s]:
+            g.wait_ge(T.sem["s" + s], cnt[s])

@@ -5,13 +5,16 @@ N, RC, NB, CAP = 8, 8192, 64, 512
 BIG = 201.0 * 2.0 ** 92
 LOW = -BIG
 SC0 = 16
+TA = 5120
+OWN1 = 4
+OWN2 = 1
 
 DT = {"f": "float32", "b": "bfloat16", "i": "int32", "u": "uint16"}
-SBUF = "tabS:8208:b Gt:4096:b SC:4112:b FS:4096:b R:512:f O:512:b P:512:b yS:64:b I:128:i E:32:i EP:4:i Es:4096:b oA:2048:b oL:1024:b Gm:512:f"
+SBUF = "tabS:8208:b Gt:4096:b SC:4112:b R:256:f O:512:b P:512:b yS:64:b I:128:i IA:128:i E:32:i EP:4:i Es:4096:b oA:2048:b oL:1024:b Gm:512:f"
 SMALL = """mx:512:b ownI:128:i ownB:128:b IF:128:f EI:128:i EF:64:b EPI:8:i inr:8:f QE:12:f Q:12:f ge:4:f KI:8:i KF:8:f io128:128:b
-im16:128:b id16:128:b ones:512:b BO:128:b Tri:128:b TriU:128:b Ob:8:f Rep:128:b S16:16:f Sel:128:f m33:32:f m32:32:f LW:512:f Sh:384:f
-Mb:136:b Cb:136:b X:128:f DP:128:b LI:64:i LF:48:f PI:48:i PF:48:f oB:512:b Tt:512:b mP:512:b off:256:u BI:12:i BF:8:f hA:512:b
-hC:128:b Fl:128:b xe:16:f xr:128:f xo:32:u"""
+im16:128:b id16:128:b ones:512:b BO:128:b Tri:128:b TriU:128:b onef:1:f Rep:128:b S16:16:f Sel:128:f m33:32:f m32:32:f
+LW:512:f Sh:384:f Mb:136:b Cb:136:b X:128:f DP:128:b LI:64:i LF:48:f PI:48:i PF:48:f oB:512:b Tt:512:b
+mP:512:b off:256:u BI:12:i BF:8:f hA:512:b hC:128:b Fl:128:b xe:16:f xr:128:f xo:32:u Mc:136:b"""
 SCRATCH, PLACE, _w = {}, {}, {}
 for _t in SBUF.split():
     _n, _c, _d = _t.split(":")
@@ -26,28 +29,27 @@ for _d in _w:
 for _i in range(8):
     SCRATCH["b%d" % _i] = ("psum", [128, 512], "float32")
     PLACE["b%d" % _i] = ("b%d" % _i, 0)
-SEMAPHORES = "sv ss sp sg dI dT dE dP dY la ld pa pd0 pd1 r1 r2 r3 sent".split()
+SCRATCH["dx"] = ("dram", [N, 128, 16], "int32")
+SEMAPHORES = "sv ss sp sg dI dE dP dX dA dY go t0 t1 ra rd la ld pa pd0 pd1 r0 r1 r2 r3 sent".split()
 CACHE = {}
 
 
 def plan(cores, topo):
     if "p" in CACHE:
         return CACHE["p"]
-    rel, far, used = {}, {}, set(cores)
+    rel, far, aid, used = {}, {}, {}, set(cores)
     for r, c in enumerate(cores):
         far[r] = [q for q in range(N) if q != r and not topo.may_write(c, cores[q])]
-        best = None
-        for x in range(512):
-            if x in used or topo.rack(topo.host(x)) == topo.rack(topo.host(c)) or topo.chip(x) != topo.chip(c):
-                continue
-            if not topo.may_write(c, x) or not all(topo.may_write(x, cores[q]) for q in far[r]):
-                continue
-            k = (topo.die(x) == topo.die(c), x)
-            if best is None or k < best:
-                best = k
-        rel[r] = best[1]
-        used.add(best[1])
-    CACHE["p"] = (rel, far)
+        mine = [x for x in range(512) if x not in used and topo.rack(topo.host(x)) != topo.rack(topo.host(c)) and topo.chip(x) == topo.chip(c)
+                and topo.may_write(c, x) and all(topo.may_write(x, cores[q]) for q in far[r])]
+        rel[r] = min(mine, key=lambda x: (topo.die(x) == topo.die(c), x))
+        used.add(rel[r])
+    for r, c in enumerate(cores):
+        near = [q for q in range(N) if q != r and q not in far[r]]
+        mine = [x for x in range(512) if x not in used and (topo.host(x), topo.chip(x)) == (topo.host(c), topo.chip(c))
+                and all(topo.may_write(x, cores[q]) for q in near)]
+        aid[r] = min(mine, key=lambda x: (topo.die(x) != topo.die(c), x))
+    CACHE["p"] = (rel, far, aid)
     return CACHE["p"]
 
 
@@ -55,13 +57,15 @@ def bits(mask, a, n):
     return sum([1 << i for i in range(16) if mask >> i & 1][a:a + n])
 
 
-def half_plan(r, far, half):
+def direct_plan(r, far, half):
     d = [q for q in range(4 * half, 4 * half + 4) if q != r and q not in far[r]]
-    out, a = [], 0
-    for q, n in zip(d, {2: [4, 4], 3: [2, 2, 4]}[len(d)]):
-        out.append((q, a, n))
-        a += n
-    return out
+    if half == 0:
+        return [[(q, 0, 8)] for q in d]
+    return [[(d[0], 0, 4), (d[1], 4, 4)]] + [[(q, 0, 8)] for q in d[2:]]
+
+
+def slots(r, far):
+    return {q: i for i, q in enumerate(far[r] + [q for q in range(N) if q != r and q not in far[r]])}
 
 
 def position(q, far):
@@ -71,43 +75,72 @@ def position(q, far):
 
 def rank_program(g, core, T, topo):
     cores = list(T.cores)
-    rel, far = plan(cores, topo)
+    rel, far, aid = plan(cores, topo)
     me = T.rank_of(core)
 
     def dst(c):
         rid, pid = topo.addr(c, core)
         return DstId(rid=rid, pnc=pid)
 
-    def xfer(src, to, dname, c0, c1, sem, eng=(0, 8)):
-        m = topo.mask(core, to[0])
-        for c in to[1:]:
-            m = m & topo.mask(core, c)
-        return RemoteDMATransfer(srcs=[src], dsts=[T[dname][:, c0:c1] for _ in to], dst_ids=[dst(c) for c in to],
-                                 dma_engine_mask=bits(m, eng[0], eng[1]), remote_sem=T.sem[sem])
+    def send(pieces, to, sem, eng=None):
+        tr, n = [], 0
+        for i, ((src, out), cs) in enumerate(zip(pieces, to)):
+            m = topo.mask(core, cs[0])
+            for c in cs[1:]:
+                m = m & topo.mask(core, c)
+            a, k = eng[i] if eng else (0, 8)
+            n += k
+            tr.append(RemoteDMATransfer(srcs=[src], dsts=[out for _ in cs], dst_ids=[dst(c) for c in cs],
+                                        dma_engine_mask=bits(m, a, k), remote_sem=T.sem[sem]))
+        g.remote_dma_fused(tr, local_sem=T.sem.sent)
+        return n
+
+    def send_direct(r, calls):
+        n, sl = 0, slots(r, far)
+        for call in calls:
+            ps = [64 * position(q, far)[r] for q, a, k in call]
+            n += send([(T.O[:, 64 * sl[q]:64 * sl[q] + 64], T.P[:, p:p + 64]) for (q, a, k), p in zip(call, ps)],
+                      [[cores[q]] for q, a, k in call], "pa", [(a, k) for q, a, k in call])
+        return n
+
+    def near_of(r):
+        return [q for q in range(N) if q != r and q not in far[r]]
 
     if me is None:
         for s in range(N):
+            x = T.R[:, 32 * s:32 * s + 32]
+            if aid[s] == core:
+                qs = [cores[q] for q in near_of(s)[OWN1:]]
+                g.wait_ge(T.sem.ra, 8)
+                n = send([(T.dx[s], T.dx[s])], [qs], "ra")
+                g.wait_ge(T.sem.la, 8)
+                n += send([(x, x)], [qs], "la")
+                g.wait_ge(T.sem.r2, 8)
+                n += send_direct(s, direct_plan(s, far, 0)[OWN2:])
+                g.wait_ge(T.sem.sent, n)
             if rel[s] == core:
-                q0, q1 = far[s]
+                qs = far[s]
+                g.wait_ge(T.sem.r0, 8)
+                send([(T.dx[s], T.dx[s])], [[cores[q] for q in qs]], "rd")
                 g.wait_ge(T.sem.r1, 8)
-                g.remote_dma_fused([xfer(T.R[:, 64 * s:64 * s + 64], [cores[q0], cores[q1]], "R", 64 * s, 64 * s + 64, "ld")], local_sem=T.sem.sent)
-                for i, q in enumerate((q0, q1)):
+                send([(x, x)], [[cores[q] for q in qs]], "ld")
+                for i, q in enumerate(qs):
                     g.wait_ge(T.sem[("r2", "r3")[i]], 8)
                     p = position(q, far)[s]
-                    g.remote_dma_fused([xfer(T.O[:, 64 * i:64 * i + 64], [cores[q]], "P", 64 * p, 64 * p + 64, "pd%d" % (p - 6))], local_sem=T.sem.sent)
-                g.wait_ge(T.sem.sent, 24)
+                    send([(T.O[:, 64 * i:64 * i + 64], T.P[:, 64 * p:64 * p + 64])], [[cores[q]]], "pd%d" % (p - 6))
+                g.wait_ge(T.sem.sent, 32)
         return
 
     Q = {"v": g.vector, "s": g.scalar, "p": g.tensor, "g": g, "y": g.sync}
     cnt = {"v": 0, "s": 0, "p": 0, "g": 0}
     seen, acc = {}, {}
 
-    def R(name, c0, c1, p0=0, p1=128, step=1):
+    def R(name, c0, c1, p0=0, p1=128):
         b, o = PLACE[name]
-        return (b, p0, p1, c0 + o, c1 + o, step)
+        return (b, p0, p1, c0 + o, c1 + o)
 
     def ap(r):
-        return T[r[0]][r[1]:r[2], r[3]:r[4]] if r[5] == 1 else T[r[0]][r[1]:r[2], r[3]:r[4]:r[5]]
+        return T[r[0]][r[1]:r[2], r[3]:r[4]]
 
     def col(name, c, p0=0, p1=128):
         return R(name, c, c + 1, p0, p1)
@@ -167,12 +200,8 @@ def rank_program(g, core, T, topo):
     def scan(out, d0, d1, ini, op0, op1):
         run("v", lambda: g.vector.tensor_tensor_scan(ap(out), ap(d0), ap(d1), val(ini), op0, op1), [out], [d0, d1] + ([ini] if isinstance(ini, tuple) else []))
 
-    def act(out, a, func, scale=1.0, bias=0.0):
-        ins = [a] + [s for s in (scale, bias) if isinstance(s, tuple)]
-        if isinstance(bias, tuple):
-            run("s", lambda: g.scalar.activation(ap(out), ap(a), func, bias=val(bias), scale=val(scale)), [out], ins)
-        else:
-            run("s", lambda: g.scalar.activation(ap(out), ap(a), func, scale=val(scale)), [out], ins)
+    def scale(out, a, s):
+        run("s", lambda: g.scalar.activation(ap(out), ap(a), F.Copy, scale=ap(s)), [out], [a, s])
 
     def mm(out, lhsT, rhs, start=True, stop=True):
         run("p", lambda: g.tensor.matmul(ap(out), ap(lhsT), ap(rhs), start, stop), [out], [lhsT, rhs])
@@ -183,7 +212,7 @@ def rank_program(g, core, T, topo):
         else:
             run("g", lambda: g.iota(ap(out), pattern, 0, cm, allow_small_or_imprecise_dtypes=True), [out], [])
 
-    def load(q, out, src, sem, v):
+    def load(q, out, src, sem, v=16):
         Q[q].dma_start(ap(out), src).then_inc(T.sem[sem], 16)
         note("d" + sem, [out], [], (sem, v))
 
@@ -193,18 +222,25 @@ def rank_program(g, core, T, topo):
         else:
             run("v", lambda: g.vector.tensor_copy(ap(out), ap(win).indirect(ap(off))), [out], [win, off])
 
-    load("y", R("I", 0, 128, 0, 16), T.idx[:, :], "dI", 16)
-    load("s", R("E", 0, 32, 0, 16), T.end[:, :], "dE", 16)
+    near = near_of(me)
+    direct = [s for s in range(N) if s not in far[me]]
+    f0, f1 = far[me]
+    ways = [aid[me]] + [cores[q] for q in near[:OWN1]]
+
+    g.scalar.dma_start(T.dx[me], T.idx[:, :]).then_inc(T.sem.dX, 16)
+    load("y", R("I", 0, 128, 0, 16), T.idx[:, :], "dI")
+    load("s", R("E", 0, 32, 0, 16), T.end[:, :], "dE")
     for w in range(4):
         load("ys"[w % 2], col("EP", w), T.end[4 * w:4 * w + 4, :], "dP", 64)
-    load("y", R("tabS", 0, RC), T.tab[:, :], "dT", 16)
+    load("y", R("tabS", 0, TA), T.tab[:, 0:TA], "t0")
 
     iota(col("KI", 0), [[0, 1]], 1)
     iota(R("im16", 0, 128), [[0, 8], [1, 16]])
     iota(R("id16", 0, 128), [[1, 8], [0, 16]])
     iota(R("io128", 0, 128), [[1, 128]])
     fill(R("ones", 0, 512), 1.0)
-    fill(R("Mb", 0, 8), 0.0)
+    fill(R("onef", 0, 1), 1.0)
+    fill(R("Mc", 0, 8), 0.0)
     fill(R("Cb", 0, 8), 0.0)
     for i, (n, op) in enumerate(((15, A.bitwise_and), (4, A.arith_shift_right), (31, A.bitwise_and), (5, A.arith_shift_right))):
         ts(col("KI", 1 + i), col("KI", 0), n, op)
@@ -213,117 +249,116 @@ def rank_program(g, core, T, topo):
     ts(R("Rep", 0, 128), R("im16", 0, 128), kp, A.is_equal)
     ts(R("S16", 0, 16), R("im16", 0, 16), kp, A.is_equal)
     ts(R("BO", 0, 128), R("id16", 0, 128), kg, A.is_equal)
-    fill(R("m33", 0, 32, 32, 33), 1.0)
-    ts(R("m33", 0, 32, 0, 32), R("io128", 0, 32, 0, 32), col("KF", 0, 0, 32), A.is_equal)
     ts(R("Tri", 0, 128), R("io128", 0, 128), kk, A.is_ge)
     tt(R("Tri", 0, 128), R("Tri", 0, 128), R("BO", 0, 128), A.mult)
-    tt(R("TriU", 0, 128), R("BO", 0, 128), R("Tri", 0, 128), A.subtract)
-    ts(col("KF", 5), kk, -1.0, A.mult, 0.5, A.add)
-    ts(col("KF", 6), kg, float(me), A.is_equal)
 
-    def selectors(c0, c1):
-        for c in range(c0, c1):
-            act(R("Es", 128 * c, 128 * c + 128, 0, 33), R("ones", 0, 128, 0, 33), F.Copy, scale=col("m33", c, 0, 33))
-
-    selectors(0, 16)
+    g.wait_ge(T.sem.dX, 16)
+    n = send([(T.dx[me], T.dx[me])], [[rel[me]]], "r0")
+    n += send([(T.dx[me], T.dx[me])], [ways], "ra")
 
     ts(R("ownI", 0, 128, 0, 16), R("I", 0, 128, 0, 16), 13, A.arith_shift_right)
     cp(R("ownB", 0, 128, 0, 16), R("ownI", 0, 128, 0, 16))
     mm(R("b0", 0, 128), R("Rep", 0, 128, 0, 16), R("ownB", 0, 128, 0, 16))
     cp(R("IF", 0, 128, 0, 16), R("I", 0, 128, 0, 16))
     mm(R("b1", 0, 16), R("IF", 0, 128, 0, 16), R("S16", 0, 16, 0, 16))
-    ts(R("EI", 0, 32, 0, 16), R("E", 0, 32, 0, 16), -1.0, A.add)
-    ts(R("EI", 32, 64, 0, 16), R("EI", 0, 32, 0, 16), 4, A.arith_shift_right)
     ts(R("Mb", 8, 136), R("b0", 0, 128), kg, A.is_equal)
     scan(R("Cb", 8, 136), R("ones", 0, 128), R("Mb", 8, 136), 0.0, A.mult, A.add)
     mm(R("b2", 0, 128), R("Tri", 0, 128), R("Mb", 8, 136), True, False)
     mm(R("b2", 0, 128), R("BO", 0, 128), R("Cb", 7, 135), False, True)
-    ts(R("EI", 64, 96, 0, 16), R("EI", 32, 64, 0, 16), float(-128 * me), A.add, -1.0, A.max)
-    ts(R("EI", 96, 128, 0, 16), R("EI", 0, 32, 0, 16), 15, A.bitwise_and)
-    ts(R("EF", 0, 32, 0, 16), R("EI", 64, 96, 0, 16), 128.0, A.min)
-    cp(R("EF", 32, 64, 0, 16), R("EI", 96, 128, 0, 16))
+    cp(R("LI", 0, 16), R("b1", 0, 16))
     tt(R("X", 0, 128), R("b2", 0, 128), R("Mb", 8, 136), A.mult)
     mm(R("b4", 0, 16), R("X", 0, 128), R("S16", 0, 16))
-    mm(R("b3", 0, 128), R("Mb", 8, 136), R("Tri", 0, 128), True, False)
-    mm(R("b3", 0, 128), R("Mb", 7, 135), R("TriU", 0, 128), False, True)
-    cp(R("LI", 0, 16), R("b1", 0, 16))
+    ts(R("LI", 48, 64), R("LI", 0, 16), 13, A.arith_shift_right)
     ts(R("LI", 16, 32), R("LI", 0, 16), 127, A.bitwise_and)
     ts(R("LI", 32, 48), R("LI", 0, 16), 7, A.arith_shift_right, 63, A.bitwise_and)
-    ts(R("LI", 48, 64), R("LI", 0, 16), 13, A.arith_shift_right)
+    ts(R("LF", 32, 48), R("LI", 48, 64), 16.0, A.mult)
     ts(R("PI", 0, 16), R("b4", 0, 16), -1.0, A.add)
+    cp(R("LF", 0, 16), R("LI", 16, 32))
     ts(R("PI", 16, 32), R("PI", 0, 16), 15, A.bitwise_and)
     ts(R("PI", 32, 48), R("PI", 0, 16), 4, A.arith_shift_right)
-    ts(R("LF", 32, 48), R("LI", 48, 64), 16.0, A.mult)
+    ts(R("LF", 16, 32), R("LI", 32, 48), -64.0, A.add, 128.0, A.mult)
     cp(R("PF", 0, 32), R("PI", 16, 48))
     tt(R("PF", 32, 48), R("PF", 0, 16), R("LF", 32, 48), A.add)
-    cp(R("LF", 0, 16), R("LI", 16, 32))
-    ts(R("LF", 16, 32), R("LI", 32, 48), -64.0, A.add, 128.0, A.mult)
-    act(R("DP", 0, 128), R("b3", 0, 128), F.Copy)
-    for h in range(2):
-        for p in range(16):
-            mm(R(("b6", "b7")[h], 32 * p, 32 * p + 32), R("Es", 128 * p, 128 * p + 128, 0, 16), R("EF", 32 * h, 32 * h + 32, 0, 16))
     for p in range(16):
         ts(R("oB", 32 * p, 32 * p + 32), R("io128", 0, 32), col("PF", 16 + p), A.is_equal)
         ts(R("oA", 128 * p, 128 * p + 128), R("io128", 0, 128), col("PF", 32 + p), A.is_equal)
-        if p == 8:
-            act(R("Tt", 0, 512), R("b6", 0, 512), F.Sign, bias=col("KF", 5))
-            mm(R("b0", 0, 512), R("DP", 0, 128), R("ones", 0, 512), True, False)
-            mm(R("b0", 0, 512), R("DP", 0, 128), R("Tt", 0, 512), False, True)
-            ts(R("mP", 0, 512), R("b7", 0, 512), kp, A.is_equal)
-            ts(R("Ob", 0, 8), R("io128", 0, 8), kg, A.is_equal)
-            ts(R("EPI", 0, 4), R("EP", 0, 4), -1.0, A.add)
-            ts(R("EPI", 4, 8), R("EPI", 0, 4), 11, A.arith_shift_right)
-            ts(R("inr", 0, 4), R("EPI", 4, 8), float(me), A.is_equal, 0.5, A.mult)
-            ts(R("inr", 4, 8), R("EPI", 4, 8), float(me), A.is_equal, float(CAP * me), A.mult)
-        if p == 12:
-            tt(R("Gm", 0, 512), R("b0", 0, 512), R("mP", 0, 512), A.mult)
-            for w in range(4):
-                mm(R("b2", 8 * w, 8 * w + 8), R("Gm", 128 * w, 128 * w + 128), R("Ob", 0, 8))
         for h in range(2):
-            act(R("oL", 64 * p + 32 * h, 64 * p + 32 * h + 32), R("oB", 32 * p, 32 * p + 32), F.Copy, scale=col("LF", 16 * h + p))
+            scale(R("oL", 64 * p + 32 * h, 64 * p + 32 * h + 32), R("oB", 32 * p, 32 * p + 32), col("LF", 16 * h + p))
         for h in range(2):
             mm(R("b5", 0, 32), R("oA", 128 * p, 128 * p + 128), R("oL", 64 * p + 32 * h, 64 * p + 32 * h + 32), p == 0 and h == 0, p == 15 and h == 1)
-    r0 = 64 * me
-    for w in range(4):
-        act(R("R", r0 + 1 + 16 * w, r0 + 16 * w + 16, step=2), R("b2", 8 * w, 8 * w + 8), F.Identity, scale=col("inr", w), bias=col("inr", 4 + w))
-    cp(R("R", r0, r0 + 63, step=2), R("b5", 0, 32))
-    selectors(16, 32)
+    fill(R("m33", 0, 32, 32, 33), 1.0)
+    ts(R("m33", 0, 32, 0, 32), R("io128", 0, 32, 0, 32), col("KF", 0, 0, 32), A.is_equal)
+    ts(R("EI", 0, 32, 0, 16), R("E", 0, 32, 0, 16), -1.0, A.add)
+    ts(R("EPI", 0, 4), R("EP", 0, 4), -1.0, A.add)
+    tt(R("TriU", 0, 128), R("BO", 0, 128), R("Tri", 0, 128), A.subtract)
+    own = R("R", 32 * me, 32 * me + 32)
+    cp(own, R("b5", 0, 32))
 
-    own = R("R", r0, r0 + 64)
     depend("g", [], [own])
-    g.remote_dma_fused([xfer(ap(own), [rel[me]], "R", r0, r0 + 64, "r1")], local_sem=T.sem.sent)
-    near = [q for q in range(N) if q != me and q not in far[me]]
-    g.remote_dma_fused([xfer(ap(own), [cores[q] for q in near], "R", r0, r0 + 64, "la")], local_sem=T.sem.sent)
+    n += send([(ap(own), ap(own))], [[rel[me]]], "r1")
+    n += send([(ap(own), ap(own))], [ways], "la")
     for s in range(N):
         if s != me:
-            note("n", [R("R", 64 * s, 64 * s + 64)], [], ("ld", 16) if s in far[me] else ("la", 8 * len(near)))
+            note("n", [R("R", 32 * s, 32 * s + 32)], [], ("ld", 16) if s in far[me] else ("la", 8 * len(near)))
+    g.sem_inc(T.sem.go, 1)
+    g.sync.wait_ge(T.sem.go, 1)
+    load("y", R("tabS", TA, RC), T.tab[:, TA:RC], "t1")
+    for s, v in (("dX", 16), ("ra", 8 * len(near)), ("rd", 16)):
+        g.sync.wait_ge(T.sem[s], v)
+    load("y", R("IA", 0, 128), T.dx[:, :, :], "dA")
 
-    ts(R("Sel", 0, 128), R("im16", 0, 128), kp, A.is_equal, col("KF", 6), A.mult)
+    for c in range(32):
+        scale(R("Es", 128 * c, 128 * c + 128, 0, 33), R("ones", 0, 128, 0, 33), col("m33", c, 0, 33))
+    ts(R("EI", 96, 128, 0, 16), R("EI", 0, 32, 0, 16), 11, A.arith_shift_right)
+    ts(R("EI", 32, 64, 0, 16), R("EI", 0, 32, 0, 16), 4, A.arith_shift_right, 127, A.bitwise_and)
+    ts(R("EI", 64, 96, 0, 16), R("EI", 0, 32, 0, 16), 15, A.bitwise_and)
+    ts(R("EI", 96, 128, 0, 16), R("EI", 96, 128, 0, 16), 16.0, A.mult)
+    cp(R("EF", 0, 32, 0, 16), R("EI", 32, 64, 0, 16))
+    tt(R("EF", 32, 64, 0, 16), R("EI", 64, 96, 0, 16), R("EI", 96, 128, 0, 16), A.add)
+    for h in range(2):
+        for p in range(16):
+            mm(R(("b6", "b7")[h], 32 * p, 32 * p + 32), R("Es", 128 * p, 128 * p + 128, 0, 16), R("EF", 32 * h, 32 * h + 32, 0, 16))
+    ts(R("EPI", 4, 8), R("EPI", 0, 4), 11, A.arith_shift_right)
+    fill(R("QE", 0, 12), 0.0)
+    ts(R("inr", 0, 4), R("EPI", 4, 8), float(CAP), A.mult, 0.0, A.max)
+    ts(R("Tt", 0, 512), R("b6", 0, 512), kk, A.is_ge)
+    ts(R("mP", 0, 512), R("b7", 0, 512), kk, A.is_equal)
+
+    ts(R("IA", 0, 128), R("IA", 0, 128), 13, A.arith_shift_right)
+    ts(R("Mc", 8, 136), R("IA", 0, 128), float(me), A.is_equal)
+    mm(R("b3", 0, 128), R("Mc", 8, 136), R("Tri", 0, 128), True, False)
+    mm(R("b3", 0, 128), R("Mc", 7, 135), R("TriU", 0, 128), False, True)
+    ts(col("KF", 6), kg, float(me), A.is_equal)
     fill(R("tabS", RC, RC + 16), LOW)
+    ts(R("Sel", 0, 128), R("im16", 0, 128), kp, A.is_equal, col("KF", 6), A.mult)
+    cp(R("DP", 0, 128), R("b3", 0, 128))
+    mm(R("b0", 0, 512), R("DP", 0, 128), R("Tt", 0, 512))
     fill(R("SC", 0, SC0), LOW)
-    fill(R("SC", 1, 2), 0.0)
-    fill(R("Fl", 0, 128, 32, 33), BIG)
     fill(col("KF", 7), BIG)
+    fill(R("Fl", 0, 128, 32, 33), BIG)
+    fill(R("SC", 1, 2), 0.0)
     ts(col("KF", 7), col("KF", 7), -2.0, A.mult)
-    ts(R("m32", 0, 32), R("io128", 0, 32), km, A.is_equal)
+    tt(R("Gm", 0, 512), R("b0", 0, 512), R("mP", 0, 512), A.mult)
     for w in range(4):
-        ts(R("LW", 128 * w, 128 * w + 128), R("im16", 0, 128), kd, A.subtract, 4.0 * w, A.is_equal)
+        mm(R("b2", w, w + 1), R("Gm", 128 * w, 128 * w + 128), R("onef", 0, 1))
+    fill(R("Q", 0, 12), 0.0)
+    cp(R("QE", 0, 4), R("EP", 0, 4))
     for i, d in enumerate((32.0, -96.0, -95.0)):
         ts(R("Sh", 128 * i, 128 * i + 128), R("io128", 0, 128), kk, A.subtract, d, A.is_equal)
+    ts(R("m32", 0, 32), R("io128", 0, 32), km, A.is_equal)
     fill(R("Sh", 256, 257), 0.0)
     fill(R("Sh", 288, 289), 0.0)
-    fill(R("QE", 0, 12), 0.0)
-    fill(R("Q", 0, 12), 0.0)
+    tt(R("Q", 0, 4), R("b2", 0, 4), R("inr", 0, 4), A.add)
+    cp(R("BI", 0, 4), R("Q", 0, 4))
+    ts(R("BI", 4, 8), R("BI", 0, 4), 127, A.bitwise_and)
+    ts(R("BI", 8, 12), R("BI", 0, 4), 7, A.arith_shift_right)
+    cp(R("BF", 0, 8), R("BI", 4, 12))
 
-    def before(q):
+    def before(q, c):
         cp(R(q, 5, 8), R(q, 0, 3))
         cp(R(q, 8, 9), R(q, 3, 4))
         for i in range(3):
-            mm(R("b7", 0, 4), R("Sh", 128 * i, 128 * i + 128), R(q, 4 * i, 4 * i + 4), i == 0, i == 2)
-
-    cp(R("QE", 0, 4), R("EP", 0, 4))
-    before("QE")
-    tt(R("ge", 0, 4), R("QE", 0, 4), R("b7", 0, 4), A.is_le)
+            mm(R("b4", c, c + 4), R("Sh", 128 * i, 128 * i + 128), R(q, 4 * i, 4 * i + 4), i == 0, i == 2)
 
     def offsets(ss, bank):
         runs = []
@@ -333,38 +368,24 @@ def rank_program(g, core, T, topo):
             else:
                 runs.append([s, s + 1])
         for a, b in runs:
-            mm(R(bank, 32 * a, 32 * b), R("Sel", 0, 128), R("R", 64 * a, 64 * b - 1, step=2))
+            mm(R(bank, 32 * a, 32 * b), R("Sel", 0, 128), R("R", 32 * a, 32 * b))
+        return runs
+
+    def convert(runs, bank):
         for a, b in runs:
             ts(R("off", 32 * a, 32 * b), R(bank, 32 * a, 32 * b), float(RC), A.add)
 
     def gather(q, s):
         indirect(q, R("Gt", CAP * s, CAP * s + CAP), R("tabS", 0, RC + 16), R("off", 32 * s, 32 * s + 32))
 
-    direct = [s for s in range(N) if s not in far[me]]
-    offsets(direct, "b1")
-    for i, s in enumerate(direct):
-        gather("sv"[i % 2], s)
-    offsets(far[me], "b4")
-    for s in far[me]:
-        gather("s", s)
-
-    for w in range(4):
-        c = 1 + 2 * (8 * w + me)
-        src, out = R("R", c, 64 * 7 + c + 1, step=64), col("Q", w)
-        run("v", lambda: g.vector.tensor_reduce(ap(out), ap(src), AxisListType.X, A.add), [out], [src])
-    before("Q")
-    cp(R("BI", 0, 4), R("Q", 0, 4))
-    ts(R("BI", 4, 8), R("BI", 0, 4), 127, A.bitwise_and)
-    ts(R("BI", 8, 12), R("BI", 0, 4), 7, A.arith_shift_right)
-    cp(R("BF", 0, 8), R("BI", 4, 12))
+    convert(offsets(direct, "b1"), "b1")
+    for s in direct:
+        if s < f1:
+            gather("s", s)
     for w in range(4):
         ts(R("hA", 128 * w, 128 * w + 128), R("io128", 0, 128), col("BF", w), A.is_equal)
         ts(R("hC", 32 * w, 32 * w + 32), R("io128", 0, 32), col("BF", 4 + w), A.is_equal)
         mm(R("b2", 0, 128, 0, 32), R("hC", 32 * w, 32 * w + 32), R("hA", 128 * w, 128 * w + 128), w == 0, w == 3)
-    tt(R("xe", 0, 4), R("Q", 0, 4), R("b7", 0, 4), A.is_gt)
-    ts(R("xe", 4, 8), R("Q", 0, 4), float(SC0 - 1), A.add)
-    tt(R("xe", 8, 12), R("xe", 0, 4), R("xe", 4, 8), A.mult)
-    tt(R("xe", 12, 16), R("xe", 8, 12), R("ge", 0, 4), A.add)
     ts(R("Fl", 0, 128, 0, 32), R("b2", 0, 128, 0, 32), 1.0, A.min, col("KF", 7, 0, 32), A.mult)
     banks = ["b0", "b3", "b5", "b6", "b7", "b1", "b4", "b0"]
 
@@ -372,62 +393,70 @@ def rank_program(g, core, T, topo):
         for c in range(4 * i, 4 * i + 4):
             mm(R(banks[i], 128 * (c % 4), 128 * (c % 4) + 128), R("Es", 128 * c, 128 * c + 128, 0, 33), R("Fl", 0, 128, 0, 33))
 
-    for i in range(4):
-        flags(i)
+    flags(0)
+    flags(1)
+    rf = offsets(far[me], "b1")
+    before("QE", 4)
+    before("Q", 0)
+    flags(2)
+    flags(3)
     for w in range(4):
-        ts(R("xr", 32 * w, 32 * w + 32), R("m32", 0, 32), col("xe", 12 + w), A.mult)
-        mm(R("b2", 0, 32), R("LW", 128 * w, 128 * w + 128), R("xr", 32 * w, 32 * w + 32), w == 0, w == 3)
+        ts(R("LW", 128 * w, 128 * w + 128), R("im16", 0, 128), kd, A.subtract, 4.0 * w, A.is_equal)
     pos = position(me, far)
-    slot = {q: i for i, q in enumerate(far[me])}
-    for q in range(N):
-        if q not in slot and q != me:
-            slot[q] = len(slot)
+    slot = slots(me, far)
 
     def piece(q):
         return R("O", 64 * slot[q], 64 * slot[q] + 64)
 
-    def take(e, q, top):
-        o = R("P", 64 * pos[me], 64 * pos[me] + 64) if q == me else piece(q)
-        indirect(e, o, R("SC", 0, SC0 + CAP * top), R("xo", 4 * q, 4 * q + 4))
-
-    def send(half):
-        q = far[me][half]
+    def stage(k, top, engines):
+        for j, q in enumerate(sorted(range(4 * k, 4 * k + 4), key=lambda q: (q not in far[me], q == me, q))):
+            o = R("P", 64 * pos[me], 64 * pos[me] + 64) if q == me else piece(q)
+            indirect(engines[j % len(engines)], o, R("SC", 0, SC0 + CAP * (top + 1)), R("xo", 4 * q, 4 * q + 4))
+        calls = direct_plan(me, far, k)
+        q = far[me][k]
         depend("g", [], [piece(q)])
-        g.remote_dma_fused([xfer(ap(piece(q)), [rel[me]], "O", 64 * half, 64 * half + 64, ("r2", "r3")[half])], local_sem=T.sem.sent)
-        tr, n = [], 0
-        for q, a, k in half_plan(me, far, half):
-            depend("g", [], [piece(q)])
-            p = position(q, far)[me]
-            tr.append(xfer(ap(piece(q)), [cores[q]], "P", 64 * p, 64 * p + 64, "pa", (a, k)))
-            n += k
-        g.remote_dma_fused(tr, local_sem=T.sem.sent)
-        return 8 + n
+        n = send([(ap(piece(q)), T.O[:, 64 * k:64 * k + 64])], [[rel[me]]], ("r2", "r3")[k])
+        if k == 0:
+            d = [slot[c[0][0]] for c in calls[OWN2:]]
+            x = R("O", 64 * min(d), 64 * max(d) + 64)
+            depend("g", [], [x])
+            n += send([(ap(x), ap(x))], [[aid[me]]], "r2")
+            calls = calls[:OWN2]
+        for c in calls:
+            for q, a, m in c:
+                depend("g", [], [piece(q)])
+        return n + send_direct(me, calls)
 
-    def order(half):
-        return sorted(range(4 * half, 4 * half + 4), key=lambda q: (q not in far[me], q == me, q))
-
-    n = 16
     for i in range(N):
         g0, g1 = CAP * i, CAP * i + CAP
-        fl = R(banks[i], 0, 512)
-        if i in (2, 4):
-            act(R("FS", g0, g1), fl, F.Copy)
-            fl = R("FS", g0, g1)
+        if i == min(f0, 1):
+            convert(rf, "b1")
+            for s in [f1] + direct:
+                if s >= f1:
+                    gather("s", s)
+        if i == f0:
+            gather("v", f0)
         last = R("SC", SC0 + g0 - 1, SC0 + g0)
-        scan(R("SC", SC0 + g0, SC0 + g1), fl, R("Gt", g0, g1), last if i else LOW, A.min, A.max)
+        scan(R("SC", SC0 + g0, SC0 + g1), R(banks[i], 0, 512), R("Gt", g0, g1), last if i else LOW, A.min, A.max)
+        if i == 2:
+            tt(R("xe", 0, 4), R("Q", 0, 4), R("b4", 0, 4), A.is_gt)
+            ts(R("xe", 4, 8), R("Q", 0, 4), float(SC0 - 1), A.add)
+            tt(R("ge", 0, 4), R("QE", 0, 4), R("b4", 4, 8), A.is_le)
+            tt(R("xe", 8, 12), R("xe", 0, 4), R("xe", 4, 8), A.mult)
+            tt(R("xe", 12, 16), R("xe", 8, 12), R("ge", 0, 4), A.add)
+            for w in range(4):
+                ts(R("xr", 32 * w, 32 * w + 32), R("m32", 0, 32), col("xe", 12 + w), A.mult)
         if i + 4 < N:
             flags(i + 4)
         if i == 2:
-            cp(R("xo", 0, 32), R("b2", 0, 32))
+            for w in range(4):
+                mm(R("b2", 0, 32), R("LW", 128 * w, 128 * w + 128), R("xr", 32 * w, 32 * w + 32), w == 0, w == 3)
         if i == 4:
-            for q in order(0):
-                take("s", q, 5)
-            n += send(0)
-    for j, q in enumerate(order(1)):
-        take("vs"[j % 2], q, 8)
-    n += send(1)
+            cp(R("xo", 0, 32), R("b2", 0, 32))
+            n += stage(0, 4, "s")
+    n += stage(1, 7, "vs")
 
-    exp = sum(k for s in range(N) for half in range(2) for q, a, k in half_plan(s, far, half) if q == me)
+    exp = sum(m for s in range(N) for k in range(2) for c in direct_plan(s, far, k) for q, a, m in c if q == me)
     note("n", [R("P", 64 * pos[s], 64 * pos[s] + 64) for s in direct if s != me], [], ("pa", exp))
     for i in range(2):
         note("n", [R("P", 64 * (6 + i), 64 * (7 + i))], [], ("pd%d" % i, 8))

@@ -5,16 +5,17 @@ N, RC, NB, CAP = 8, 8192, 64, 512
 BIG = 201.0 * 2.0 ** 92
 LOW = -BIG
 SC0 = 16
-TA = 5120
-OWN1 = 4
+NT = 8
+OWN1 = 3
 OWN2 = 1
 
 DT = {"f": "float32", "b": "bfloat16", "i": "int32", "u": "uint16"}
-SBUF = "tabS:8208:b Gt:4096:b SC:4112:b R:256:f O:512:b P:512:b yS:64:b I:128:i IA:128:i E:32:i EP:4:i Es:4096:b oA:2048:b oL:1024:b Gm:512:f"
-SMALL = """mx:512:b ownI:128:i ownB:128:b IF:128:f EI:128:i EF:64:b EPI:8:i inr:8:f QE:12:f Q:12:f ge:4:f KI:8:i KF:8:f io128:128:b
-im16:128:b id16:128:b ones:512:b BO:128:b Tri:128:b TriU:128:b onef:1:f Rep:128:b S16:16:f Sel:128:f m33:32:f m32:32:f
-LW:512:f Sh:384:f Mb:136:b Cb:136:b X:128:f DP:128:b LI:64:i LF:48:f PI:48:i PF:48:f oB:512:b Tt:512:b
-mP:512:b off:256:u BI:12:i BF:8:f hA:512:b hC:128:b Fl:128:b xe:16:f xr:128:f xo:32:u Mc:136:b"""
+SBUF = """tabS:8208:b Gt:4096:b SC:4112:b R:256:f O:512:b P:512:b yS:64:b I:128:i IA:128:i E:32:i EP:4:i Es:4096:b oA:2048:b oL:1024:b
+Gm:512:f Fl:128:b xo:32:u EF:64:b ER:1024:b"""
+SMALL = """mx:512:b ownI:128:i ownB:128:b IF:128:f EI:128:i EPI:8:i inr:8:f QE:12:f Q:12:f ge:4:f KI:8:i KF:8:f io128:128:b
+im16:128:i id16:128:i ioI:128:i ones:512:b BO:128:b Tri:128:b TriU:128:b onef:1:f Rep:128:b S16:16:f Sel:128:f m32:32:f
+LW:512:f Sh:384:f Mb:136:b Cb:136:b X:128:f DP:128:b LI:64:i LF:48:f PI:48:i PF:48:f Tt:512:b
+mP:512:b off:256:u BI:12:i BF:8:f hA:512:b hC:128:b xe:16:f xr:128:f Mc:136:b"""
 SCRATCH, PLACE, _w = {}, {}, {}
 for _t in SBUF.split():
     _n, _c, _d = _t.split(":")
@@ -30,14 +31,16 @@ for _i in range(8):
     SCRATCH["b%d" % _i] = ("psum", [128, 512], "float32")
     PLACE["b%d" % _i] = ("b%d" % _i, 0)
 SCRATCH["dx"] = ("dram", [N, 128, 16], "int32")
-SEMAPHORES = "sv ss sp sg dI dE dP dX dA dY go t0 t1 ra rd la ld pa pd0 pd1 r0 r1 r2 r3 sent".split()
+SCRATCH["de"] = ("dram", [128, 4], "int32")
+SEMAPHORES = "sv ss sp sg dI dE dP dX dA dR dS dY ra rd rq fl px pa pd0 pd1 r0 r1 r2 r3 sent".split()
+SEMAPHORES += ["t%d" % _i for _i in range(NT)] + ["l%d" % _i for _i in range(N)]
 CACHE = {}
 
 
 def plan(cores, topo):
     if "p" in CACHE:
         return CACHE["p"]
-    rel, far, aid, used = {}, {}, {}, set(cores)
+    rel, far, aid, scr, used = {}, {}, {}, {}, set(cores)
     for r, c in enumerate(cores):
         far[r] = [q for q in range(N) if q != r and not topo.may_write(c, cores[q])]
         mine = [x for x in range(512) if x not in used and topo.rack(topo.host(x)) != topo.rack(topo.host(c)) and topo.chip(x) == topo.chip(c)
@@ -49,7 +52,12 @@ def plan(cores, topo):
         mine = [x for x in range(512) if x not in used and (topo.host(x), topo.chip(x)) == (topo.host(c), topo.chip(c))
                 and all(topo.may_write(x, cores[q]) for q in near)]
         aid[r] = min(mine, key=lambda x: (topo.die(x) != topo.die(c), x))
-    CACHE["p"] = (rel, far, aid)
+        used.add(aid[r])
+    for r, c in enumerate(cores):
+        mine = [x for x in range(512) if x not in used and (topo.host(x), topo.chip(x)) == (topo.host(c), topo.chip(c))]
+        scr[r] = min(mine, key=lambda x: (topo.die(x) != topo.die(c), x))
+        used.add(scr[r])
+    CACHE["p"] = (rel, far, aid, scr)
     return CACHE["p"]
 
 
@@ -75,7 +83,7 @@ def position(q, far):
 
 def rank_program(g, core, T, topo):
     cores = list(T.cores)
-    rel, far, aid = plan(cores, topo)
+    rel, far, aid, scr = plan(cores, topo)
     me = T.rank_of(core)
 
     def dst(c):
@@ -104,26 +112,30 @@ def rank_program(g, core, T, topo):
         return n
 
     def near_of(r):
-        return [q for q in range(N) if q != r and q not in far[r]]
+        return sorted([q for q in range(N) if q != r and q not in far[r]], key=lambda q: (q - r) % N)
 
-    if me is None:
+    def raw_ways(r):
+        a = [q for q in near_of(r) if topo.may_write(scr[r], scr[q])][-1]
+        b = [q for q in near_of(r) if q != a]
+        return a, b[-1], b[:-1]
+
+    if me is None and core not in scr.values():
         for s in range(N):
             x = T.R[:, 32 * s:32 * s + 32]
             if aid[s] == core:
-                qs = [cores[q] for q in near_of(s)[OWN1:]]
                 g.wait_ge(T.sem.ra, 8)
-                n = send([(T.dx[s], T.dx[s])], [qs], "ra")
-                g.wait_ge(T.sem.la, 8)
-                n += send([(x, x)], [qs], "la")
+                n = send([(T.dx[s], T.dx[s])], [[scr[raw_ways(s)[1]]]], "ra")
+                g.wait_ge(T.sem["l%d" % s], 8)
+                n += send([(x, x)], [[cores[q] for q in near_of(s)[OWN1:]]], "l%d" % s)
                 g.wait_ge(T.sem.r2, 8)
                 n += send_direct(s, direct_plan(s, far, 0)[OWN2:])
                 g.wait_ge(T.sem.sent, n)
             if rel[s] == core:
                 qs = far[s]
                 g.wait_ge(T.sem.r0, 8)
-                send([(T.dx[s], T.dx[s])], [[cores[q] for q in qs]], "rd")
+                send([(T.dx[s], T.dx[s])], [[scr[q] for q in qs]], "rd")
                 g.wait_ge(T.sem.r1, 8)
-                send([(x, x)], [[cores[q] for q in qs]], "ld")
+                send([(x, x)], [[cores[q] for q in qs]], "l%d" % s)
                 for i, q in enumerate(qs):
                     g.wait_ge(T.sem[("r2", "r3")[i]], 8)
                     p = position(q, far)[s]
@@ -207,10 +219,7 @@ def rank_program(g, core, T, topo):
         run("p", lambda: g.tensor.matmul(ap(out), ap(lhsT), ap(rhs), start, stop), [out], [lhsT, rhs])
 
     def iota(out, pattern, cm=0):
-        if SCRATCH[out[0]][2] == "int32":
-            run("g", lambda: g.iota(ap(out), pattern, 0, cm), [out], [])
-        else:
-            run("g", lambda: g.iota(ap(out), pattern, 0, cm, allow_small_or_imprecise_dtypes=True), [out], [])
+        run("g", lambda: g.iota(ap(out), pattern, 0, cm), [out], [])
 
     def load(q, out, src, sem, v=16):
         Q[q].dma_start(ap(out), src).then_inc(T.sem[sem], 16)
@@ -222,45 +231,171 @@ def rank_program(g, core, T, topo):
         else:
             run("v", lambda: g.vector.tensor_copy(ap(out), ap(win).indirect(ap(off))), [out], [win, off])
 
+    def finish(n):
+        g.wait_ge(T.sem.sent, n)
+        for s in "vspg":
+            if seen.get(("g", "s" + s), 0) < cnt[s]:
+                g.wait_ge(T.sem["s" + s], cnt[s])
+
+    kk, kp, kg, km, kd = [col("KF", i) for i in range(5)]
+
+    def numbers():
+        iota(col("KI", 0), [[0, 1]], 1)
+        iota(R("ioI", 0, 128), [[1, 128]])
+
+    def coordinates():
+        for i, (n, op) in enumerate(((15, A.bitwise_and), (4, A.arith_shift_right), (31, A.bitwise_and), (5, A.arith_shift_right))):
+            ts(col("KI", 1 + i), col("KI", 0), n, op)
+        cp(R("KF", 0, 5), R("KI", 0, 5))
+        ts(R("im16", 0, 128), R("ioI", 0, 128), 15, A.bitwise_and)
+
+    def columns():
+        cp(R("io128", 0, 128), R("ioI", 0, 128))
+        ts(R("id16", 0, 128), R("ioI", 0, 128), 4, A.arith_shift_right)
+
+    def triangle():
+        ts(R("BO", 0, 128), R("id16", 0, 128), kg, A.is_equal)
+        ts(R("Tri", 0, 128), R("io128", 0, 128), kk, A.is_ge)
+        tt(R("Tri", 0, 128), R("Tri", 0, 128), R("BO", 0, 128), A.mult)
+
+    def choose(c):
+        scale(R("Es", 128 * c, 128 * c + 128, 0, 32), R("ones", 0, 128, 0, 32), col("m32", c, 0, 32))
+
+    if me is None:
+        w0 = [s for s in range(N) if scr[s] == core][0]
+        for q in (g.sync, g.scalar):
+            q.wait_ge(T.sem.rq, 8)
+        load("y", R("E", 0, 32, 0, 16), T.de[:, :], "dE")
+        for w in range(4):
+            load("sy"[w % 2], col("EP", w), T.de[32 * w:32 * w + 32, :], "dP", 64)
+        numbers()
+        g.wait_ge(T.sem.r0, 8)
+        n = send([(T.dx[w0], T.dx[w0])], [[scr[raw_ways(w0)[0]]]], "ra")
+        fill(R("ones", 0, 512), 1.0)
+        fill(R("onef", 0, 1), 1.0)
+        fill(R("Mc", 0, 8), 0.0)
+        fill(R("Fl", 0, 128), BIG)
+        fill(R("xo", 0, 32), 0)
+        fill(R("QE", 0, 12), 0.0)
+        fill(R("Q", 0, 12), 0.0)
+        coordinates()
+        columns()
+        fill(col("KF", 7), BIG)
+        ts(col("KF", 7), col("KF", 7), -2.0, A.mult)
+        triangle()
+        tt(R("TriU", 0, 128), R("BO", 0, 128), R("Tri", 0, 128), A.subtract)
+        ts(R("m32", 0, 32), R("io128", 0, 32), km, A.is_equal)
+        for i, d in enumerate((32.0, -96.0, -95.0)):
+            ts(R("Sh", 128 * i, 128 * i + 128), R("io128", 0, 128), kk, A.subtract, d, A.is_equal)
+        fill(R("Sh", 256, 257), 0.0)
+        fill(R("Sh", 288, 289), 0.0)
+        for w in range(4):
+            ts(R("LW", 128 * w, 128 * w + 128), R("im16", 0, 128), kd, A.subtract, 4.0 * w, A.is_equal)
+        ts(R("EI", 0, 32, 0, 16), R("E", 0, 32, 0, 16), -1.0, A.add)
+        ts(R("EI", 96, 128, 0, 16), R("EI", 0, 32, 0, 16), 11, A.arith_shift_right)
+        ts(R("EI", 32, 64, 0, 16), R("EI", 0, 32, 0, 16), 4, A.arith_shift_right, 127, A.bitwise_and)
+        ts(R("EI", 64, 96, 0, 16), R("EI", 0, 32, 0, 16), 15, A.bitwise_and)
+        ts(R("EI", 96, 128, 0, 16), R("EI", 96, 128, 0, 16), 16.0, A.mult)
+        cp(R("EF", 0, 32, 0, 16), R("EI", 32, 64, 0, 16))
+        tt(R("EF", 32, 64, 0, 16), R("EI", 64, 96, 0, 16), R("EI", 96, 128, 0, 16), A.add)
+        for h in range(2):
+            depend("y", [], [R("EF", 32 * h, 32 * h + 32, 0, 16)])
+            load("y", R("ER", 512 * h, 512 * h + 512, 0, 1), ap(R("EF", 32 * h, 32 * h + 32, 0, 16)), ("dR", "dS")[h])
+        g.sync.wait_ge(T.sem.r0, 8)
+        g.sync.wait_ge(T.sem.ra, 8 * len(near_of(w0)))
+        g.sync.wait_ge(T.sem.rd, 16)
+        load("y", R("IA", 0, 128), T.dx[:, :, :], "dA")
+
+        def before(q, c):
+            cp(R(q, 5, 8), R(q, 0, 3))
+            cp(R(q, 8, 9), R(q, 3, 4))
+            for i in range(3):
+                mm(R(("b4", "b5")[c // 4], c, c + 4), R("Sh", 128 * i, 128 * i + 128), R(q, 4 * i, 4 * i + 4), i == 0, i == 2)
+
+        cp(R("QE", 0, 4), R("EP", 0, 4))
+        before("QE", 4)
+        tt(R("ge", 0, 4), R("QE", 0, 4), R("b5", 4, 8), A.is_le)
+        ts(R("EPI", 0, 4), R("EP", 0, 4), -1.0, A.add)
+        ts(R("EPI", 4, 8), R("EPI", 0, 4), 11, A.arith_shift_right)
+        ts(R("inr", 0, 4), R("EPI", 4, 8), float(CAP), A.mult, 0.0, A.max)
+        for h in range(2):
+            mm(R(("b6", "b7")[h], 0, 512), R("ones", 0, 128, 0, 1), R("ER", 512 * h, 512 * h + 512, 0, 1))
+        ts(R("Tt", 0, 512), R("b6", 0, 512), kk, A.is_ge)
+        ts(R("mP", 0, 512), R("b7", 0, 512), kk, A.is_equal)
+        ts(R("IA", 0, 128), R("IA", 0, 128), 13, A.arith_shift_right)
+        ts(R("Mc", 8, 136), R("IA", 0, 128), float(w0), A.is_equal)
+        mm(R("b3", 0, 128), R("Mc", 8, 136), R("Tri", 0, 128), True, False)
+        mm(R("b3", 0, 128), R("Mc", 7, 135), R("TriU", 0, 128), False, True)
+        cp(R("DP", 0, 128), R("b3", 0, 128))
+        for w in range(4):
+            x = R(("b0", "b1", "b5", "b7")[w], 0, 128)
+            y = R("Gm", 128 * w, 128 * w + 128)
+            mm(x, R("DP", 0, 128), R("Tt", 128 * w, 128 * w + 128))
+            tt(y, x, R("mP", 128 * w, 128 * w + 128), A.mult)
+        for w in range(4):
+            mm(R("b2", w, w + 1), R("Gm", 128 * w, 128 * w + 128), R("onef", 0, 1))
+        tt(R("BI", 0, 4), R("b2", 0, 4), R("inr", 0, 4), A.add)
+        ts(R("BI", 4, 8), R("BI", 0, 4), 127, A.bitwise_and)
+        ts(R("BI", 8, 12), R("BI", 0, 4), 7, A.arith_shift_right)
+        cp(R("BF", 0, 8), R("BI", 4, 12))
+        for w in range(4):
+            ts(R("hA", 128 * w, 128 * w + 128), R("io128", 0, 128), col("BF", w), A.is_equal)
+            ts(R("hC", 32 * w, 32 * w + 32), R("io128", 0, 32), col("BF", 4 + w), A.is_equal)
+            mm(R("b0", 0, 128, 0, 32), R("hC", 32 * w, 32 * w + 32), R("hA", 128 * w, 128 * w + 128), w == 0, w == 3)
+        ts(R("Fl", 0, 128, 0, 32), R("b0", 0, 128, 0, 32), col("KF", 7, 0, 32), A.mult, BIG, A.add)
+        depend("g", [], [R("Fl", 0, 128)])
+        n += send([(T.Fl[:, :], T.Fl[:, :])], [[cores[w0]]], "fl")
+        cp(R("Q", 0, 4), R("BI", 0, 4))
+        before("Q", 0)
+        tt(R("xe", 0, 4), R("Q", 0, 4), R("b4", 0, 4), A.is_gt)
+        ts(R("xe", 4, 8), R("Q", 0, 4), float(SC0 - 1), A.add)
+        tt(R("xe", 8, 12), R("xe", 0, 4), R("xe", 4, 8), A.mult)
+        tt(R("xe", 12, 16), R("xe", 8, 12), R("ge", 0, 4), A.add)
+        for w in range(4):
+            ts(R("xr", 32 * w, 32 * w + 32), R("m32", 0, 32), col("xe", 12 + w), A.mult)
+            mm(R("b2", 0, 32), R("LW", 128 * w, 128 * w + 128), R("xr", 32 * w, 32 * w + 32), w == 0, w == 3)
+        cp(R("xo", 0, 32), R("b2", 0, 32))
+        depend("g", [], [R("xo", 0, 32)])
+        n += send([(T.xo[:, :], T.xo[:, :])], [[cores[w0]]], "px")
+        finish(n)
+        return
+
     near = near_of(me)
-    direct = [s for s in range(N) if s not in far[me]]
     f0, f1 = far[me]
-    ways = [aid[me]] + [cores[q] for q in near[:OWN1]]
 
     g.scalar.dma_start(T.dx[me], T.idx[:, :]).then_inc(T.sem.dX, 16)
     load("y", R("I", 0, 128, 0, 16), T.idx[:, :], "dI")
-    load("s", R("E", 0, 32, 0, 16), T.end[:, :], "dE")
-    for w in range(4):
-        load("ys"[w % 2], col("EP", w), T.end[4 * w:4 * w + 4, :], "dP", 64)
-    load("y", R("tabS", 0, TA), T.tab[:, 0:TA], "t0")
+    g.scalar.dma_start(T.de[:, :], T.end[:, :]).then_inc(T.sem.dE, 16)
+    for i in range(NT):
+        a, b = RC // NT * i, RC // NT * (i + 1)
+        if i > 1:
+            g.sync.wait_ge(T.sem["t%d" % (i - 2)], 16)
+        load("y", R("tabS", a, b), T.tab[:, a:b], "t%d" % i)
 
-    iota(col("KI", 0), [[0, 1]], 1)
-    iota(R("im16", 0, 128), [[0, 8], [1, 16]])
-    iota(R("id16", 0, 128), [[1, 8], [0, 16]])
-    iota(R("io128", 0, 128), [[1, 128]])
+    numbers()
     fill(R("ones", 0, 512), 1.0)
-    fill(R("onef", 0, 1), 1.0)
-    fill(R("Mc", 0, 8), 0.0)
     fill(R("Cb", 0, 8), 0.0)
-    for i, (n, op) in enumerate(((15, A.bitwise_and), (4, A.arith_shift_right), (31, A.bitwise_and), (5, A.arith_shift_right))):
-        ts(col("KI", 1 + i), col("KI", 0), n, op)
-    cp(R("KF", 0, 5), R("KI", 0, 5))
-    kk, kp, kg, km, kd = [col("KF", i) for i in range(5)]
-    ts(R("Rep", 0, 128), R("im16", 0, 128), kp, A.is_equal)
+    coordinates()
+    ts(R("Rep", 0, 128, 0, 16), R("im16", 0, 128, 0, 16), col("KF", 1, 0, 16), A.is_equal)
     ts(R("S16", 0, 16), R("im16", 0, 16), kp, A.is_equal)
-    ts(R("BO", 0, 128), R("id16", 0, 128), kg, A.is_equal)
-    ts(R("Tri", 0, 128), R("io128", 0, 128), kk, A.is_ge)
-    tt(R("Tri", 0, 128), R("Tri", 0, 128), R("BO", 0, 128), A.mult)
 
     g.wait_ge(T.sem.dX, 16)
-    n = send([(T.dx[me], T.dx[me])], [[rel[me]]], "r0")
-    n += send([(T.dx[me], T.dx[me])], [ways], "ra")
+    x = (T.dx[me], T.dx[me])
+    n = send([x, x], [[rel[me]], [scr[me]]], "r0", [(0, 8), (8, 8)])
+    g.wait_ge(T.sem.dE, 16)
+    n += send([(T.de[:, :], T.de[:, :])], [[scr[me]]], "rq", [(8, 8)])
+    n += send([x, x], [[scr[q] for q in raw_ways(me)[2]], [aid[me]]], "ra", [(0, 8), (8, 8)])
 
     ts(R("ownI", 0, 128, 0, 16), R("I", 0, 128, 0, 16), 13, A.arith_shift_right)
     cp(R("ownB", 0, 128, 0, 16), R("ownI", 0, 128, 0, 16))
     mm(R("b0", 0, 128), R("Rep", 0, 128, 0, 16), R("ownB", 0, 128, 0, 16))
     cp(R("IF", 0, 128, 0, 16), R("I", 0, 128, 0, 16))
     mm(R("b1", 0, 16), R("IF", 0, 128, 0, 16), R("S16", 0, 16, 0, 16))
+    columns()
+    triangle()
+    ts(R("m32", 0, 32), R("io128", 0, 32), km, A.is_equal)
+    for c in range(32):
+        choose(c)
     ts(R("Mb", 8, 136), R("b0", 0, 128), kg, A.is_equal)
     scan(R("Cb", 8, 136), R("ones", 0, 128), R("Mb", 8, 136), 0.0, A.mult, A.add)
     mm(R("b2", 0, 128), R("Tri", 0, 128), R("Mb", 8, 136), True, False)
@@ -280,128 +415,52 @@ def rank_program(g, core, T, topo):
     cp(R("PF", 0, 32), R("PI", 16, 48))
     tt(R("PF", 32, 48), R("PF", 0, 16), R("LF", 32, 48), A.add)
     for p in range(16):
-        ts(R("oB", 32 * p, 32 * p + 32), R("io128", 0, 32), col("PF", 16 + p), A.is_equal)
         ts(R("oA", 128 * p, 128 * p + 128), R("io128", 0, 128), col("PF", 32 + p), A.is_equal)
         for h in range(2):
-            scale(R("oL", 64 * p + 32 * h, 64 * p + 32 * h + 32), R("oB", 32 * p, 32 * p + 32), col("LF", 16 * h + p))
-        for h in range(2):
+            ts(R("oL", 64 * p + 32 * h, 64 * p + 32 * h + 32), R("io128", 0, 32), col("PF", 16 + p), A.is_equal, col("LF", 16 * h + p), A.mult)
             mm(R("b5", 0, 32), R("oA", 128 * p, 128 * p + 128), R("oL", 64 * p + 32 * h, 64 * p + 32 * h + 32), p == 0 and h == 0, p == 15 and h == 1)
-    fill(R("m33", 0, 32, 32, 33), 1.0)
-    ts(R("m33", 0, 32, 0, 32), R("io128", 0, 32, 0, 32), col("KF", 0, 0, 32), A.is_equal)
-    ts(R("EI", 0, 32, 0, 16), R("E", 0, 32, 0, 16), -1.0, A.add)
-    ts(R("EPI", 0, 4), R("EP", 0, 4), -1.0, A.add)
-    tt(R("TriU", 0, 128), R("BO", 0, 128), R("Tri", 0, 128), A.subtract)
     own = R("R", 32 * me, 32 * me + 32)
     cp(own, R("b5", 0, 32))
 
     depend("g", [], [own])
     n += send([(ap(own), ap(own))], [[rel[me]]], "r1")
-    n += send([(ap(own), ap(own))], [ways], "la")
+    x = (ap(own), ap(own))
+    n += send([x, x], [[cores[q] for q in near[:OWN1]], [aid[me]]], "l%d" % me, [(0, 8), (8, 8)])
     for s in range(N):
         if s != me:
-            note("n", [R("R", 32 * s, 32 * s + 32)], [], ("ld", 16) if s in far[me] else ("la", 8 * len(near)))
-    g.sem_inc(T.sem.go, 1)
-    g.sync.wait_ge(T.sem.go, 1)
-    load("y", R("tabS", TA, RC), T.tab[:, TA:RC], "t1")
-    for s, v in (("dX", 16), ("ra", 8 * len(near)), ("rd", 16)):
-        g.sync.wait_ge(T.sem[s], v)
-    load("y", R("IA", 0, 128), T.dx[:, :, :], "dA")
+            note("n", [R("R", 32 * s, 32 * s + 32)], [], ("l%d" % s, 8))
+    note("n", [R("Fl", 0, 128)], [], ("fl", 8))
+    note("n", [R("xo", 0, 32)], [], ("px", 8))
 
-    for c in range(32):
-        scale(R("Es", 128 * c, 128 * c + 128, 0, 33), R("ones", 0, 128, 0, 33), col("m33", c, 0, 33))
-    ts(R("EI", 96, 128, 0, 16), R("EI", 0, 32, 0, 16), 11, A.arith_shift_right)
-    ts(R("EI", 32, 64, 0, 16), R("EI", 0, 32, 0, 16), 4, A.arith_shift_right, 127, A.bitwise_and)
-    ts(R("EI", 64, 96, 0, 16), R("EI", 0, 32, 0, 16), 15, A.bitwise_and)
-    ts(R("EI", 96, 128, 0, 16), R("EI", 96, 128, 0, 16), 16.0, A.mult)
-    cp(R("EF", 0, 32, 0, 16), R("EI", 32, 64, 0, 16))
-    tt(R("EF", 32, 64, 0, 16), R("EI", 64, 96, 0, 16), R("EI", 96, 128, 0, 16), A.add)
-    for h in range(2):
-        for p in range(16):
-            mm(R(("b6", "b7")[h], 32 * p, 32 * p + 32), R("Es", 128 * p, 128 * p + 128, 0, 16), R("EF", 32 * h, 32 * h + 32, 0, 16))
-    ts(R("EPI", 4, 8), R("EPI", 0, 4), 11, A.arith_shift_right)
-    fill(R("QE", 0, 12), 0.0)
-    ts(R("inr", 0, 4), R("EPI", 4, 8), float(CAP), A.mult, 0.0, A.max)
-    ts(R("Tt", 0, 512), R("b6", 0, 512), kk, A.is_ge)
-    ts(R("mP", 0, 512), R("b7", 0, 512), kk, A.is_equal)
-
-    ts(R("IA", 0, 128), R("IA", 0, 128), 13, A.arith_shift_right)
-    ts(R("Mc", 8, 136), R("IA", 0, 128), float(me), A.is_equal)
-    mm(R("b3", 0, 128), R("Mc", 8, 136), R("Tri", 0, 128), True, False)
-    mm(R("b3", 0, 128), R("Mc", 7, 135), R("TriU", 0, 128), False, True)
     ts(col("KF", 6), kg, float(me), A.is_equal)
-    fill(R("tabS", RC, RC + 16), LOW)
     ts(R("Sel", 0, 128), R("im16", 0, 128), kp, A.is_equal, col("KF", 6), A.mult)
-    cp(R("DP", 0, 128), R("b3", 0, 128))
-    mm(R("b0", 0, 512), R("DP", 0, 128), R("Tt", 0, 512))
-    fill(R("SC", 0, SC0), LOW)
-    fill(col("KF", 7), BIG)
-    fill(R("Fl", 0, 128, 32, 33), BIG)
-    fill(R("SC", 1, 2), 0.0)
-    ts(col("KF", 7), col("KF", 7), -2.0, A.mult)
-    tt(R("Gm", 0, 512), R("b0", 0, 512), R("mP", 0, 512), A.mult)
-    for w in range(4):
-        mm(R("b2", w, w + 1), R("Gm", 128 * w, 128 * w + 128), R("onef", 0, 1))
-    fill(R("Q", 0, 12), 0.0)
-    cp(R("QE", 0, 4), R("EP", 0, 4))
-    for i, d in enumerate((32.0, -96.0, -95.0)):
-        ts(R("Sh", 128 * i, 128 * i + 128), R("io128", 0, 128), kk, A.subtract, d, A.is_equal)
-    ts(R("m32", 0, 32), R("io128", 0, 32), km, A.is_equal)
-    fill(R("Sh", 256, 257), 0.0)
-    fill(R("Sh", 288, 289), 0.0)
-    tt(R("Q", 0, 4), R("b2", 0, 4), R("inr", 0, 4), A.add)
-    cp(R("BI", 0, 4), R("Q", 0, 4))
-    ts(R("BI", 4, 8), R("BI", 0, 4), 127, A.bitwise_and)
-    ts(R("BI", 8, 12), R("BI", 0, 4), 7, A.arith_shift_right)
-    cp(R("BF", 0, 8), R("BI", 4, 12))
+    fill(R("tabS", RC, RC + 16), LOW)
 
-    def before(q, c):
-        cp(R(q, 5, 8), R(q, 0, 3))
-        cp(R(q, 8, 9), R(q, 3, 4))
-        for i in range(3):
-            mm(R("b4", c, c + 4), R("Sh", 128 * i, 128 * i + 128), R(q, 4 * i, 4 * i + 4), i == 0, i == 2)
-
-    def offsets(ss, bank):
-        runs = []
-        for s in ss:
-            if runs and runs[-1][1] == s:
-                runs[-1][1] = s + 1
-            else:
-                runs.append([s, s + 1])
-        for a, b in runs:
-            mm(R(bank, 32 * a, 32 * b), R("Sel", 0, 128), R("R", 32 * a, 32 * b))
-        return runs
-
-    def convert(runs, bank):
-        for a, b in runs:
-            ts(R("off", 32 * a, 32 * b), R(bank, 32 * a, 32 * b), float(RC), A.add)
+    def offsets(s, bank):
+        mm(R(bank, 32 * s, 32 * s + 32), R("Sel", 0, 128), R("R", 32 * s, 32 * s + 32))
+        ts(R("off", 32 * s, 32 * s + 32), R(bank, 32 * s, 32 * s + 32), float(RC), A.add)
 
     def gather(q, s):
         indirect(q, R("Gt", CAP * s, CAP * s + CAP), R("tabS", 0, RC + 16), R("off", 32 * s, 32 * s + 32))
 
-    convert(offsets(direct, "b1"), "b1")
-    for s in direct:
-        if s < f1:
-            gather("s", s)
-    for w in range(4):
-        ts(R("hA", 128 * w, 128 * w + 128), R("io128", 0, 128), col("BF", w), A.is_equal)
-        ts(R("hC", 32 * w, 32 * w + 32), R("io128", 0, 32), col("BF", 4 + w), A.is_equal)
-        mm(R("b2", 0, 128, 0, 32), R("hC", 32 * w, 32 * w + 32), R("hA", 128 * w, 128 * w + 128), w == 0, w == 3)
-    ts(R("Fl", 0, 128, 0, 32), R("b2", 0, 128, 0, 32), 1.0, A.min, col("KF", 7, 0, 32), A.mult)
-    banks = ["b0", "b3", "b5", "b6", "b7", "b1", "b4", "b0"]
+    offsets(me, "b1")
+    fill(R("SC", 0, SC0), LOW)
+    fill(R("SC", 1, 2), 0.0)
+    gather("v", me)
+    order = sorted(near, key=lambda s: (near_of(s).index(me), s))
+    order.insert(4, f0)
+    order.append(f1)
+    for i, s in enumerate(order):
+        offsets(s, ("b4", "b1")[i % 2])
+        gather("v" if s in (order[1], f0) else "s", s)
+    banks = ["b0", "b2", "b3", "b5", "b6", "b7", "b0", "b2"]
 
     def flags(i):
         for c in range(4 * i, 4 * i + 4):
-            mm(R(banks[i], 128 * (c % 4), 128 * (c % 4) + 128), R("Es", 128 * c, 128 * c + 128, 0, 33), R("Fl", 0, 128, 0, 33))
+            mm(R(banks[i], 128 * (c % 4), 128 * (c % 4) + 128), R("Es", 128 * c, 128 * c + 128, 0, 32), R("Fl", 0, 128, 0, 32))
 
-    flags(0)
-    flags(1)
-    rf = offsets(far[me], "b1")
-    before("QE", 4)
-    before("Q", 0)
-    flags(2)
-    flags(3)
-    for w in range(4):
-        ts(R("LW", 128 * w, 128 * w + 128), R("im16", 0, 128), kd, A.subtract, 4.0 * w, A.is_equal)
+    for i in range(6):
+        flags(i)
     pos = position(me, far)
     slot = slots(me, far)
 
@@ -429,35 +488,16 @@ def rank_program(g, core, T, topo):
 
     for i in range(N):
         g0, g1 = CAP * i, CAP * i + CAP
-        if i == min(f0, 1):
-            convert(rf, "b1")
-            for s in [f1] + direct:
-                if s >= f1:
-                    gather("s", s)
-        if i == f0:
-            gather("v", f0)
         last = R("SC", SC0 + g0 - 1, SC0 + g0)
         scan(R("SC", SC0 + g0, SC0 + g1), R(banks[i], 0, 512), R("Gt", g0, g1), last if i else LOW, A.min, A.max)
-        if i == 2:
-            tt(R("xe", 0, 4), R("Q", 0, 4), R("b4", 0, 4), A.is_gt)
-            ts(R("xe", 4, 8), R("Q", 0, 4), float(SC0 - 1), A.add)
-            tt(R("ge", 0, 4), R("QE", 0, 4), R("b4", 4, 8), A.is_le)
-            tt(R("xe", 8, 12), R("xe", 0, 4), R("xe", 4, 8), A.mult)
-            tt(R("xe", 12, 16), R("xe", 8, 12), R("ge", 0, 4), A.add)
-            for w in range(4):
-                ts(R("xr", 32 * w, 32 * w + 32), R("m32", 0, 32), col("xe", 12 + w), A.mult)
-        if i + 4 < N:
-            flags(i + 4)
-        if i == 2:
-            for w in range(4):
-                mm(R("b2", 0, 32), R("LW", 128 * w, 128 * w + 128), R("xr", 32 * w, 32 * w + 32), w == 0, w == 3)
+        if i + 6 < N:
+            flags(i + 6)
         if i == 4:
-            cp(R("xo", 0, 32), R("b2", 0, 32))
             n += stage(0, 4, "s")
     n += stage(1, 7, "vs")
 
     exp = sum(m for s in range(N) for k in range(2) for c in direct_plan(s, far, k) for q, a, m in c if q == me)
-    note("n", [R("P", 64 * pos[s], 64 * pos[s] + 64) for s in direct if s != me], [], ("pa", exp))
+    note("n", [R("P", 64 * pos[s], 64 * pos[s] + 64) for s in range(N) if s not in far[me] and s != me], [], ("pa", exp))
     for i in range(2):
         note("n", [R("P", 64 * (6 + i), 64 * (7 + i))], [], ("pd%d" % i, 8))
     tt(R("mx", 0, 192), R("P", 0, 192), R("P", 192, 384), A.max)
@@ -468,7 +508,4 @@ def rank_program(g, core, T, topo):
     depend("y", [], [R("yS", 0, 64)])
     g.sync.dma_start(T.y[:, :], T.yS[:, :]).then_inc(T.sem.dY, 16)
     g.sync.wait_ge(T.sem.dY, 16)
-    g.wait_ge(T.sem.sent, n)
-    for s in "vspg":
-        if seen.get(("g", "s" + s), 0) < cnt[s]:
-            g.wait_ge(T.sem["s" + s], cnt[s])
+    finish(n)

from concourse.bass import DstId, RemoteDMATransfer
from concourse.mybir import dt, AluOpType as A, AxisListType, ActivationFunctionType as F

N, RC, NB, CAP = 8, 8192, 64, 512
BIG = 201.0 * 2.0 ** 92
LOW = -BIG
SC0 = 16
NT = 8
OWN1 = 3
OWN2 = 1

DT = {"f": "float32", "b": "bfloat16", "i": "int32", "u": "uint16"}
SBUF = """tabS:8208:b Gt:4096:b SC:4112:b R:256:f O:512:b P:512:b yS:64:b I:128:i IA:128:i E:32:i EP:4:i Es:4096:b oA:2048:b oL:1024:b
Gm:512:f Fl:128:b xo:32:u EF:64:b ER:1024:b"""
SMALL = """mx:512:b ownI:128:i ownB:128:b IF:128:f EI:128:i EPI:8:i inr:8:f QE:12:f Q:12:f ge:4:f KI:8:i KF:8:f io128:128:b
im16:128:i id16:128:i ioI:128:i ones:512:b BO:128:b Tri:128:b TriU:128:b onef:1:f Rep:128:b S16:16:f Sel:128:f m32:32:f
LW:512:f Sh:384:f Mb:136:b Cb:136:b X:128:f DP:128:b LI:64:i LF:48:f PI:48:i PF:48:f Tt:512:b
mP:512:b off:256:u BI:12:i BF:8:f hA:512:b hC:128:b xe:16:f xr:128:f Mc:136:b"""
SCRATCH, PLACE, _w = {}, {}, {}
for _t in SBUF.split():
    _n, _c, _d = _t.split(":")
    SCRATCH[_n] = ("sbuf", [128, int(_c)], DT[_d])
    PLACE[_n] = (_n, 0)
for _t in SMALL.split():
    _n, _c, _d = _t.split(":")
    PLACE[_n] = ("small_" + _d, _w.get(_d, 0))
    _w[_d] = _w.get(_d, 0) + (int(_c) + 15) // 16 * 16
for _d in _w:
    SCRATCH["small_" + _d] = ("sbuf", [128, _w[_d]], DT[_d])
for _i in range(8):
    SCRATCH["b%d" % _i] = ("psum", [128, 512], "float32")
    PLACE["b%d" % _i] = ("b%d" % _i, 0)
SCRATCH["dx"] = ("dram", [N, 128, 16], "int32")
SCRATCH["de"] = ("dram", [128, 4], "int32")
SEMAPHORES = "sv ss sp sg dI dE dP dX dA dR dS dY ra rd rq fl px pa pd0 pd1 r0 r1 r2 r3 sent".split()
SEMAPHORES += ["t%d" % _i for _i in range(NT)] + ["l%d" % _i for _i in range(N)]
CACHE = {}


def plan(cores, topo):
    if "p" in CACHE:
        return CACHE["p"]
    rel, far, aid, scr, used = {}, {}, {}, {}, set(cores)
    for r, c in enumerate(cores):
        far[r] = [q for q in range(N) if q != r and not topo.may_write(c, cores[q])]
        mine = [x for x in range(512) if x not in used and topo.rack(topo.host(x)) != topo.rack(topo.host(c)) and topo.chip(x) == topo.chip(c)
                and topo.may_write(c, x) and all(topo.may_write(x, cores[q]) for q in far[r])]
        rel[r] = min(mine, key=lambda x: (topo.die(x) == topo.die(c), x))
        used.add(rel[r])
    for r, c in enumerate(cores):
        near = [q for q in range(N) if q != r and q not in far[r]]
        mine = [x for x in range(512) if x not in used and (topo.host(x), topo.chip(x)) == (topo.host(c), topo.chip(c))
                and all(topo.may_write(x, cores[q]) for q in near)]
        aid[r] = min(mine, key=lambda x: (topo.die(x) != topo.die(c), x))
        used.add(aid[r])
    for r, c in enumerate(cores):
        mine = [x for x in range(512) if x not in used and (topo.host(x), topo.chip(x)) == (topo.host(c), topo.chip(c))]
        scr[r] = min(mine, key=lambda x: (topo.die(x) != topo.die(c), x))
        used.add(scr[r])
    CACHE["p"] = (rel, far, aid, scr)
    return CACHE["p"]


def bits(mask, a, n):
    return sum([1 << i for i in range(16) if mask >> i & 1][a:a + n])


def direct_plan(r, far, half):
    d = [q for q in range(4 * half, 4 * half + 4) if q != r and q not in far[r]]
    if half == 0:
        return [[(q, 0, 8)] for q in d]
    return [[(d[0], 0, 4), (d[1], 4, 4)]] + [[(q, 0, 8)] for q in d[2:]]


def slots(r, far):
    return {q: i for i, q in enumerate(far[r] + [q for q in range(N) if q != r and q not in far[r]])}


def position(q, far):
    near = [s for s in range(N) if s not in far[q]]
    return {s: i for i, s in enumerate(near + far[q])}


def rank_program(g, core, T, topo):
    cores = list(T.cores)
    rel, far, aid, scr = plan(cores, topo)
    me = T.rank_of(core)

    def dst(c):
        rid, pid = topo.addr(c, core)
        return DstId(rid=rid, pnc=pid)

    def send(pieces, to, sem, eng=None):
        tr, n = [], 0
        for i, ((src, out), cs) in enumerate(zip(pieces, to)):
            m = topo.mask(core, cs[0])
            for c in cs[1:]:
                m = m & topo.mask(core, c)
            a, k = eng[i] if eng else (0, 8)
            n += k
            tr.append(RemoteDMATransfer(srcs=[src], dsts=[out for _ in cs], dst_ids=[dst(c) for c in cs],
                                        dma_engine_mask=bits(m, a, k), remote_sem=T.sem[sem]))
        g.remote_dma_fused(tr, local_sem=T.sem.sent)
        return n

    def send_direct(r, calls):
        n, sl = 0, slots(r, far)
        for call in calls:
            ps = [64 * position(q, far)[r] for q, a, k in call]
            n += send([(T.O[:, 64 * sl[q]:64 * sl[q] + 64], T.P[:, p:p + 64]) for (q, a, k), p in zip(call, ps)],
                      [[cores[q]] for q, a, k in call], "pa", [(a, k) for q, a, k in call])
        return n

    def near_of(r):
        return sorted([q for q in range(N) if q != r and q not in far[r]], key=lambda q: (q - r) % N)

    def raw_ways(r):
        a = [q for q in near_of(r) if topo.may_write(scr[r], scr[q])][-1]
        b = [q for q in near_of(r) if q != a]
        return a, b[-1], b[:-1]

    if me is None and core not in scr.values():
        for s in range(N):
            x = T.R[:, 32 * s:32 * s + 32]
            if aid[s] == core:
                g.wait_ge(T.sem.ra, 8)
                n = send([(T.dx[s], T.dx[s])], [[scr[raw_ways(s)[1]]]], "ra")
                g.wait_ge(T.sem["l%d" % s], 8)
                n += send([(x, x)], [[cores[q] for q in near_of(s)[OWN1:]]], "l%d" % s)
                g.wait_ge(T.sem.r2, 8)
                n += send_direct(s, direct_plan(s, far, 0)[OWN2:])
                g.wait_ge(T.sem.sent, n)
            if rel[s] == core:
                qs = far[s]
                g.wait_ge(T.sem.r0, 8)
                send([(T.dx[s], T.dx[s])], [[scr[q] for q in qs]], "rd")
                g.wait_ge(T.sem.r1, 8)
                send([(x, x)], [[cores[q] for q in qs]], "l%d" % s)
                for i, q in enumerate(qs):
                    g.wait_ge(T.sem[("r2", "r3")[i]], 8)
                    p = position(q, far)[s]
                    send([(T.O[:, 64 * i:64 * i + 64], T.P[:, 64 * p:64 * p + 64])], [[cores[q]]], "pd%d" % (p - 6))
                g.wait_ge(T.sem.sent, 32)
        return

    Q = {"v": g.vector, "s": g.scalar, "p": g.tensor, "g": g, "y": g.sync}
    cnt = {"v": 0, "s": 0, "p": 0, "g": 0}
    seen, acc = {}, {}

    def R(name, c0, c1, p0=0, p1=128):
        b, o = PLACE[name]
        return (b, p0, p1, c0 + o, c1 + o)

    def ap(r):
        return T[r[0]][r[1]:r[2], r[3]:r[4]]

    def col(name, c, p0=0, p1=128):
        return R(name, c, c + 1, p0, p1)

    def depend(q, outs, ins):
        want = {}
        for kind, regs in (("w", outs), ("r", ins)):
            for r in regs:
                bank = SCRATCH[r[0]][0] == "psum"
                for (r2, k2, tok, q2) in acc.get(r[0], []):
                    if bank and q2 != q:
                        hit = True
                    elif bank and q == "p":
                        hit = False
                    else:
                        hit = r[1] < r2[2] and r2[1] < r[2] and r[3] < r2[4] and r2[3] < r[4] and (kind == "w" or k2 == "w")
                        if q == q2 and k2 == "r":
                            hit = False
                    if hit and want.get(tok[0], 0) < tok[1]:
                        want[tok[0]] = tok[1]
        for s in want:
            if seen.get((q, s), 0) < want[s]:
                Q[q].wait_ge(T.sem[s], want[s])
                seen[(q, s)] = want[s]

    def note(q, outs, ins, tok):
        for kind, regs in (("w", outs), ("r", ins)):
            for r in regs:
                acc.setdefault(r[0], []).append((r, kind, tok, q))

    def run(q, fn, outs, ins):
        depend(q, outs, ins)
        cnt[q] += 1
        tok = ("s" + q, cnt[q])
        fn().then_inc(T.sem[tok[0]], 1)
        note(q, outs, ins, tok)

    def val(x):
        return ap(x) if isinstance(x, tuple) else x

    def ts(out, in0, s1, op0, s2=None, op1=None):
        ins = [in0] + [s for s in (s1, s2) if isinstance(s, tuple)]
        if op1 is None:
            run("v", lambda: g.vector.tensor_scalar(ap(out), ap(in0), val(s1), None, op0), [out], ins)
        else:
            run("v", lambda: g.vector.tensor_scalar(ap(out), ap(in0), val(s1), val(s2), op0, op1), [out], ins)

    def tt(out, a, b, op):
        run("v", lambda: g.vector.tensor_tensor(ap(out), ap(a), ap(b), op), [out], [a, b])

    def cp(out, a):
        run("v", lambda: g.vector.tensor_copy(ap(out), ap(a)), [out], [a])

    def fill(r, c):
        run("v", lambda: g.vector.memset(ap(r), c), [r], [])

    def scan(out, d0, d1, ini, op0, op1):
        run("v", lambda: g.vector.tensor_tensor_scan(ap(out), ap(d0), ap(d1), val(ini), op0, op1), [out], [d0, d1] + ([ini] if isinstance(ini, tuple) else []))

    def scale(out, a, s):
        run("s", lambda: g.scalar.activation(ap(out), ap(a), F.Copy, scale=ap(s)), [out], [a, s])

    def mm(out, lhsT, rhs, start=True, stop=True):
        run("p", lambda: g.tensor.matmul(ap(out), ap(lhsT), ap(rhs), start, stop), [out], [lhsT, rhs])

    def iota(out, pattern, cm=0):
        run("g", lambda: g.iota(ap(out), pattern, 0, cm), [out], [])

    def load(q, out, src, sem, v=16):
        Q[q].dma_start(ap(out), src).then_inc(T.sem[sem], 16)
        note("d" + sem, [out], [], (sem, v))

    def indirect(q, out, win, off):
        if q == "s":
            run("s", lambda: g.scalar.activation(ap(out), ap(win).indirect(ap(off)), F.Copy), [out], [win, off])
        else:
            run("v", lambda: g.vector.tensor_copy(ap(out), ap(win).indirect(ap(off))), [out], [win, off])

    def finish(n):
        g.wait_ge(T.sem.sent, n)
        for s in "vspg":
            if seen.get(("g", "s" + s), 0) < cnt[s]:
                g.wait_ge(T.sem["s" + s], cnt[s])

    kk, kp, kg, km, kd = [col("KF", i) for i in range(5)]

    def numbers():
        iota(col("KI", 0), [[0, 1]], 1)
        iota(R("ioI", 0, 128), [[1, 128]])

    def coordinates():
        for i, (n, op) in enumerate(((15, A.bitwise_and), (4, A.arith_shift_right), (31, A.bitwise_and), (5, A.arith_shift_right))):
            ts(col("KI", 1 + i), col("KI", 0), n, op)
        cp(R("KF", 0, 5), R("KI", 0, 5))
        ts(R("im16", 0, 128), R("ioI", 0, 128), 15, A.bitwise_and)

    def columns():
        cp(R("io128", 0, 128), R("ioI", 0, 128))
        ts(R("id16", 0, 128), R("ioI", 0, 128), 4, A.arith_shift_right)

    def triangle():
        ts(R("BO", 0, 128), R("id16", 0, 128), kg, A.is_equal)
        ts(R("Tri", 0, 128), R("io128", 0, 128), kk, A.is_ge)
        tt(R("Tri", 0, 128), R("Tri", 0, 128), R("BO", 0, 128), A.mult)

    def choose(c):
        scale(R("Es", 128 * c, 128 * c + 128, 0, 32), R("ones", 0, 128, 0, 32), col("m32", c, 0, 32))

    if me is None:
        w0 = [s for s in range(N) if scr[s] == core][0]
        for q in (g.sync, g.scalar):
            q.wait_ge(T.sem.rq, 8)
        load("y", R("E", 0, 32, 0, 16), T.de[:, :], "dE")
        for w in range(4):
            load("sy"[w % 2], col("EP", w), T.de[32 * w:32 * w + 32, :], "dP", 64)
        numbers()
        g.wait_ge(T.sem.r0, 8)
        n = send([(T.dx[w0], T.dx[w0])], [[scr[raw_ways(w0)[0]]]], "ra")
        fill(R("ones", 0, 512), 1.0)
        fill(R("onef", 0, 1), 1.0)
        fill(R("Mc", 0, 8), 0.0)
        fill(R("Fl", 0, 128), BIG)
        fill(R("xo", 0, 32), 0)
        fill(R("QE", 0, 12), 0.0)
        fill(R("Q", 0, 12), 0.0)
        coordinates()
        columns()
        fill(col("KF", 7), BIG)
        ts(col("KF", 7), col("KF", 7), -2.0, A.mult)
        triangle()
        tt(R("TriU", 0, 128), R("BO", 0, 128), R("Tri", 0, 128), A.subtract)
        ts(R("m32", 0, 32), R("io128", 0, 32), km, A.is_equal)
        for i, d in enumerate((32.0, -96.0, -95.0)):
            ts(R("Sh", 128 * i, 128 * i + 128), R("io128", 0, 128), kk, A.subtract, d, A.is_equal)
        fill(R("Sh", 256, 257), 0.0)
        fill(R("Sh", 288, 289), 0.0)
        for w in range(4):
            ts(R("LW", 128 * w, 128 * w + 128), R("im16", 0, 128), kd, A.subtract, 4.0 * w, A.is_equal)
        ts(R("EI", 0, 32, 0, 16), R("E", 0, 32, 0, 16), -1.0, A.add)
        ts(R("EI", 96, 128, 0, 16), R("EI", 0, 32, 0, 16), 11, A.arith_shift_right)
        ts(R("EI", 32, 64, 0, 16), R("EI", 0, 32, 0, 16), 4, A.arith_shift_right, 127, A.bitwise_and)
        ts(R("EI", 64, 96, 0, 16), R("EI", 0, 32, 0, 16), 15, A.bitwise_and)
        ts(R("EI", 96, 128, 0, 16), R("EI", 96, 128, 0, 16), 16.0, A.mult)
        cp(R("EF", 0, 32, 0, 16), R("EI", 32, 64, 0, 16))
        tt(R("EF", 32, 64, 0, 16), R("EI", 64, 96, 0, 16), R("EI", 96, 128, 0, 16), A.add)
        for h in range(2):
            depend("y", [], [R("EF", 32 * h, 32 * h + 32, 0, 16)])
            load("y", R("ER", 512 * h, 512 * h + 512, 0, 1), ap(R("EF", 32 * h, 32 * h + 32, 0, 16)), ("dR", "dS")[h])
        g.sync.wait_ge(T.sem.r0, 8)
        g.sync.wait_ge(T.sem.ra, 8 * len(near_of(w0)))
        g.sync.wait_ge(T.sem.rd, 16)
        load("y", R("IA", 0, 128), T.dx[:, :, :], "dA")

        def before(q, c):
            cp(R(q, 5, 8), R(q, 0, 3))
            cp(R(q, 8, 9), R(q, 3, 4))
            for i in range(3):
                mm(R(("b4", "b5")[c // 4], c, c + 4), R("Sh", 128 * i, 128 * i + 128), R(q, 4 * i, 4 * i + 4), i == 0, i == 2)

        cp(R("QE", 0, 4), R("EP", 0, 4))
        before("QE", 4)
        tt(R("ge", 0, 4), R("QE", 0, 4), R("b5", 4, 8), A.is_le)
        ts(R("EPI", 0, 4), R("EP", 0, 4), -1.0, A.add)
        ts(R("EPI", 4, 8), R("EPI", 0, 4), 11, A.arith_shift_right)
        ts(R("inr", 0, 4), R("EPI", 4, 8), float(CAP), A.mult, 0.0, A.max)
        for h in range(2):
            mm(R(("b6", "b7")[h], 0, 512), R("ones", 0, 128, 0, 1), R("ER", 512 * h, 512 * h + 512, 0, 1))
        ts(R("Tt", 0, 512), R("b6", 0, 512), kk, A.is_ge)
        ts(R("mP", 0, 512), R("b7", 0, 512), kk, A.is_equal)
        ts(R("IA", 0, 128), R("IA", 0, 128), 13, A.arith_shift_right)
        ts(R("Mc", 8, 136), R("IA", 0, 128), float(w0), A.is_equal)
        mm(R("b3", 0, 128), R("Mc", 8, 136), R("Tri", 0, 128), True, False)
        mm(R("b3", 0, 128), R("Mc", 7, 135), R("TriU", 0, 128), False, True)
        cp(R("DP", 0, 128), R("b3", 0, 128))
        for w in range(4):
            x = R(("b0", "b1", "b5", "b7")[w], 0, 128)
            y = R("Gm", 128 * w, 128 * w + 128)
            mm(x, R("DP", 0, 128), R("Tt", 128 * w, 128 * w + 128))
            tt(y, x, R("mP", 128 * w, 128 * w + 128), A.mult)
        for w in range(4):
            mm(R("b2", w, w + 1), R("Gm", 128 * w, 128 * w + 128), R("onef", 0, 1))
        tt(R("BI", 0, 4), R("b2", 0, 4), R("inr", 0, 4), A.add)
        ts(R("BI", 4, 8), R("BI", 0, 4), 127, A.bitwise_and)
        ts(R("BI", 8, 12), R("BI", 0, 4), 7, A.arith_shift_right)
        cp(R("BF", 0, 8), R("BI", 4, 12))
        for w in range(4):
            ts(R("hA", 128 * w, 128 * w + 128), R("io128", 0, 128), col("BF", w), A.is_equal)
            ts(R("hC", 32 * w, 32 * w + 32), R("io128", 0, 32), col("BF", 4 + w), A.is_equal)
            mm(R("b0", 0, 128, 0, 32), R("hC", 32 * w, 32 * w + 32), R("hA", 128 * w, 128 * w + 128), w == 0, w == 3)
        ts(R("Fl", 0, 128, 0, 32), R("b0", 0, 128, 0, 32), col("KF", 7, 0, 32), A.mult, BIG, A.add)
        depend("g", [], [R("Fl", 0, 128)])
        n += send([(T.Fl[:, :], T.Fl[:, :])], [[cores[w0]]], "fl")
        cp(R("Q", 0, 4), R("BI", 0, 4))
        before("Q", 0)
        tt(R("xe", 0, 4), R("Q", 0, 4), R("b4", 0, 4), A.is_gt)
        ts(R("xe", 4, 8), R("Q", 0, 4), float(SC0 - 1), A.add)
        tt(R("xe", 8, 12), R("xe", 0, 4), R("xe", 4, 8), A.mult)
        tt(R("xe", 12, 16), R("xe", 8, 12), R("ge", 0, 4), A.add)
        for w in range(4):
            ts(R("xr", 32 * w, 32 * w + 32), R("m32", 0, 32), col("xe", 12 + w), A.mult)
            mm(R("b2", 0, 32), R("LW", 128 * w, 128 * w + 128), R("xr", 32 * w, 32 * w + 32), w == 0, w == 3)
        cp(R("xo", 0, 32), R("b2", 0, 32))
        depend("g", [], [R("xo", 0, 32)])
        n += send([(T.xo[:, :], T.xo[:, :])], [[cores[w0]]], "px")
        finish(n)
        return

    near = near_of(me)
    f0, f1 = far[me]

    g.scalar.dma_start(T.dx[me], T.idx[:, :]).then_inc(T.sem.dX, 16)
    load("y", R("I", 0, 128, 0, 16), T.idx[:, :], "dI")
    g.scalar.dma_start(T.de[:, :], T.end[:, :]).then_inc(T.sem.dE, 16)
    for i in range(NT):
        a, b = RC // NT * i, RC // NT * (i + 1)
        if i > 1:
            g.sync.wait_ge(T.sem["t%d" % (i - 2)], 16)
        load("y", R("tabS", a, b), T.tab[:, a:b], "t%d" % i)

    numbers()
    fill(R("ones", 0, 512), 1.0)
    fill(R("Cb", 0, 8), 0.0)
    coordinates()
    ts(R("Rep", 0, 128, 0, 16), R("im16", 0, 128, 0, 16), col("KF", 1, 0, 16), A.is_equal)
    ts(R("S16", 0, 16), R("im16", 0, 16), kp, A.is_equal)

    g.wait_ge(T.sem.dX, 16)
    x = (T.dx[me], T.dx[me])
    n = send([x, x], [[rel[me]], [scr[me]]], "r0", [(0, 8), (8, 8)])
    g.wait_ge(T.sem.dE, 16)
    n += send([(T.de[:, :], T.de[:, :])], [[scr[me]]], "rq", [(8, 8)])
    n += send([x, x], [[scr[q] for q in raw_ways(me)[2]], [aid[me]]], "ra", [(0, 8), (8, 8)])

    ts(R("ownI", 0, 128, 0, 16), R("I", 0, 128, 0, 16), 13, A.arith_shift_right)
    cp(R("ownB", 0, 128, 0, 16), R("ownI", 0, 128, 0, 16))
    mm(R("b0", 0, 128), R("Rep", 0, 128, 0, 16), R("ownB", 0, 128, 0, 16))
    cp(R("IF", 0, 128, 0, 16), R("I", 0, 128, 0, 16))
    mm(R("b1", 0, 16), R("IF", 0, 128, 0, 16), R("S16", 0, 16, 0, 16))
    columns()
    triangle()
    ts(R("m32", 0, 32), R("io128", 0, 32), km, A.is_equal)
    for c in range(32):
        choose(c)
    ts(R("Mb", 8, 136), R("b0", 0, 128), kg, A.is_equal)
    scan(R("Cb", 8, 136), R("ones", 0, 128), R("Mb", 8, 136), 0.0, A.mult, A.add)
    mm(R("b2", 0, 128), R("Tri", 0, 128), R("Mb", 8, 136), True, False)
    mm(R("b2", 0, 128), R("BO", 0, 128), R("Cb", 7, 135), False, True)
    cp(R("LI", 0, 16), R("b1", 0, 16))
    tt(R("X", 0, 128), R("b2", 0, 128), R("Mb", 8, 136), A.mult)
    mm(R("b4", 0, 16), R("X", 0, 128), R("S16", 0, 16))
    ts(R("LI", 48, 64), R("LI", 0, 16), 13, A.arith_shift_right)
    ts(R("LI", 16, 32), R("LI", 0, 16), 127, A.bitwise_and)
    ts(R("LI", 32, 48), R("LI", 0, 16), 7, A.arith_shift_right, 63, A.bitwise_and)
    ts(R("LF", 32, 48), R("LI", 48, 64), 16.0, A.mult)
    ts(R("PI", 0, 16), R("b4", 0, 16), -1.0, A.add)
    cp(R("LF", 0, 16), R("LI", 16, 32))
    ts(R("PI", 16, 32), R("PI", 0, 16), 15, A.bitwise_and)
    ts(R("PI", 32, 48), R("PI", 0, 16), 4, A.arith_shift_right)
    ts(R("LF", 16, 32), R("LI", 32, 48), -64.0, A.add, 128.0, A.mult)
    cp(R("PF", 0, 32), R("PI", 16, 48))
    tt(R("PF", 32, 48), R("PF", 0, 16), R("LF", 32, 48), A.add)
    for p in range(16):
        ts(R("oA", 128 * p, 128 * p + 128), R("io128", 0, 128), col("PF", 32 + p), A.is_equal)
        for h in range(2):
            ts(R("oL", 64 * p + 32 * h, 64 * p + 32 * h + 32), R("io128", 0, 32), col("PF", 16 + p), A.is_equal, col("LF", 16 * h + p), A.mult)
            mm(R("b5", 0, 32), R("oA", 128 * p, 128 * p + 128), R("oL", 64 * p + 32 * h, 64 * p + 32 * h + 32), p == 0 and h == 0, p == 15 and h == 1)
    own = R("R", 32 * me, 32 * me + 32)
    cp(own, R("b5", 0, 32))

    depend("g", [], [own])
    n += send([(ap(own), ap(own))], [[rel[me]]], "r1")
    x = (ap(own), ap(own))
    n += send([x, x], [[cores[q] for q in near[:OWN1]], [aid[me]]], "l%d" % me, [(0, 8), (8, 8)])
    for s in range(N):
        if s != me:
            note("n", [R("R", 32 * s, 32 * s + 32)], [], ("l%d" % s, 8))
    note("n", [R("Fl", 0, 128)], [], ("fl", 8))
    note("n", [R("xo", 0, 32)], [], ("px", 8))

    ts(col("KF", 6), kg, float(me), A.is_equal)
    ts(R("Sel", 0, 128), R("im16", 0, 128), kp, A.is_equal, col("KF", 6), A.mult)
    fill(R("tabS", RC, RC + 16), LOW)

    def offsets(s, bank):
        mm(R(bank, 32 * s, 32 * s + 32), R("Sel", 0, 128), R("R", 32 * s, 32 * s + 32))
        ts(R("off", 32 * s, 32 * s + 32), R(bank, 32 * s, 32 * s + 32), float(RC), A.add)

    def gather(q, s):
        indirect(q, R("Gt", CAP * s, CAP * s + CAP), R("tabS", 0, RC + 16), R("off", 32 * s, 32 * s + 32))

    offsets(me, "b1")
    fill(R("SC", 0, SC0), LOW)
    fill(R("SC", 1, 2), 0.0)
    gather("v", me)
    order = sorted(near, key=lambda s: (near_of(s).index(me), s))
    order.insert(4, f0)
    order.append(f1)
    for i, s in enumerate(order):
        offsets(s, ("b4", "b1")[i % 2])
        gather("v" if s in (order[1], f0) else "s", s)
    banks = ["b0", "b2", "b3", "b5", "b6", "b7", "b0", "b2"]

    def flags(i):
        for c in range(4 * i, 4 * i + 4):
            mm(R(banks[i], 128 * (c % 4), 128 * (c % 4) + 128), R("Es", 128 * c, 128 * c + 128, 0, 32), R("Fl", 0, 128, 0, 32))

    for i in range(6):
        flags(i)
    pos = position(me, far)
    slot = slots(me, far)

    def piece(q):
        return R("O", 64 * slot[q], 64 * slot[q] + 64)

    def stage(k, top, engines):
        for j, q in enumerate(sorted(range(4 * k, 4 * k + 4), key=lambda q: (q not in far[me], q == me, q))):
            o = R("P", 64 * pos[me], 64 * pos[me] + 64) if q == me else piece(q)
            indirect(engines[j % len(engines)], o, R("SC", 0, SC0 + CAP * (top + 1)), R("xo", 4 * q, 4 * q + 4))
        calls = direct_plan(me, far, k)
        q = far[me][k]
        depend("g", [], [piece(q)])
        n = send([(ap(piece(q)), T.O[:, 64 * k:64 * k + 64])], [[rel[me]]], ("r2", "r3")[k])
        if k == 0:
            d = [slot[c[0][0]] for c in calls[OWN2:]]
            x = R("O", 64 * min(d), 64 * max(d) + 64)
            depend("g", [], [x])
            n += send([(ap(x), ap(x))], [[aid[me]]], "r2")
            calls = calls[:OWN2]
        for c in calls:
            for q, a, m in c:
                depend("g", [], [piece(q)])
        return n + send_direct(me, calls)

    for i in range(N):
        g0, g1 = CAP * i, CAP * i + CAP
        last = R("SC", SC0 + g0 - 1, SC0 + g0)
        scan(R("SC", SC0 + g0, SC0 + g1), R(banks[i], 0, 512), R("Gt", g0, g1), last if i else LOW, A.min, A.max)
        if i + 6 < N:
            flags(i + 6)
        if i == 4:
            n += stage(0, 4, "s")
    n += stage(1, 7, "vs")

    exp = sum(m for s in range(N) for k in range(2) for c in direct_plan(s, far, k) for q, a, m in c if q == me)
    note("n", [R("P", 64 * pos[s], 64 * pos[s] + 64) for s in range(N) if s not in far[me] and s != me], [], ("pa", exp))
    for i in range(2):
        note("n", [R("P", 64 * (6 + i), 64 * (7 + i))], [], ("pd%d" % i, 8))
    tt(R("mx", 0, 192), R("P", 0, 192), R("P", 192, 384), A.max)
    tt(R("mx", 192, 256), R("mx", 0, 64), R("mx", 64, 128), A.max)
    tt(R("mx", 256, 320), R("mx", 192, 256), R("mx", 128, 192), A.max)
    tt(R("mx", 320, 384), R("P", 384, 448), R("P", 448, 512), A.max)
    tt(R("yS", 0, 64), R("mx", 256, 320), R("mx", 320, 384), A.max)
    depend("y", [], [R("yS", 0, 64)])
    g.sync.dma_start(T.y[:, :], T.yS[:, :]).then_inc(T.sem.dY, 16)
    g.sync.wait_ge(T.sem.dY, 16)
    finish(n)
